import numpy as np
import ml_dtypes


def mxq(x, axis, fmt="e4m3"):
    dtype, down = {"e4m3": (ml_dtypes.float8_e4m3fn, 7), "e5m2": (ml_dtypes.float8_e5m2, 14)}[fmt]
    v = np.moveaxis(np.asarray(x, np.float32).astype(ml_dtypes.bfloat16).astype(np.float64), axis, -1)
    blocks = v.reshape(v.shape[:-1] + (-1, 32))
    amax = np.abs(blocks).max(-1, keepdims=True)
    byte = np.maximum(np.where(amax > 0, np.frexp(amax)[1] - 1 + 127, 0) - down, 1)
    scale = np.exp2(byte - 127.0)
    codes = (blocks / scale).astype(np.float32).astype(dtype).astype(np.float64)
    return np.moveaxis((codes * scale).reshape(v.shape), -1, axis)


WIDE = False


def mx_kscale(k):
    if not WIDE:
        return np.ones(k)
    levels = np.array([10, -10, 5, -5, 0])
    if k % 512:
        return np.exp2(np.random.permutation(np.resize(levels, k // 32))).repeat(32)
    a = np.empty((k // 512, 16))
    for p in range(k // 512):
        a[p, :8] = np.random.permutation(np.resize(levels, 8))
        for g in range(8):
            far = levels[np.abs(levels - a[p, g]) >= 10]
            a[p, g + 8] = far[np.random.randint(len(far))]
    return np.exp2(a.ravel()).repeat(32)


BF16 = ml_dtypes.bfloat16


def bf(x):
    return np.asarray(x, np.float32).astype(BF16)


def f64(x):
    return np.asarray(x).astype(np.float64)

def planes(Y):
    n, m = Y.shape
    b = f64(bf(Y)).reshape(n // 32, 32, m)
    amax = np.abs(b).max(1)
    byte = np.clip(np.where(amax > 0, np.frexp(amax)[1] - 1 + 127 - 7, 1), 1, 254)
    codes = (b * np.exp2(127.0 - byte)[:, None, :]).reshape(n, m).astype(np.float32).astype(ml_dtypes.float8_e4m3fn).view(np.uint8)
    words = codes.reshape(n // 512, 128, 4, m).transpose(0, 1, 3, 2)
    return np.ascontiguousarray(words), np.ascontiguousarray(byte.astype(np.uint8).reshape(n // 512, 16, m))


N, D, R, E = 512, 1024, 512, 4


def softmax(a):
    e = np.exp(a - a.max(-1, keepdims=True))
    return e / e.sum(-1, keepdims=True)


def setup_inputs():
    s, t = mx_kscale(D), mx_kscale(R)
    return {
        "x0": bf(np.random.standard_normal((N, D))),
        "xl": bf(np.random.standard_normal((N, D)) * s),
        "v": bf(np.random.standard_normal((E, D, R)) / np.sqrt(D) / s[:, None]),
        "c": bf((1.0 + 0.3 * np.random.standard_normal((E, R))) * t),
        "u": bf(np.random.standard_normal((E, R, D)) / np.sqrt(R) / t[:, None]),
        "gate": bf(np.random.standard_normal((D, E)) / np.sqrt(D) / s[:, None]),
        "b": bf(np.random.standard_normal(D) * 0.3),
    }


def expert_outputs(xl, v, c, u):
    p = np.tanh(mxq(xl, 1, "e4m3") @ mxq(v, 1, "e4m3"))
    q = p * c[:, None, :]
    return mxq(q, 2, "e4m3") @ mxq(u, 1, "e4m3")


def core(x0, xl, v, c, u, gate, b):
    x0, xl, v, c, u, gate, b = f64(x0), f64(xl), f64(v), f64(c), f64(u), f64(gate), f64(b)
    z = expert_outputs(xl, v, c, u)
    g = softmax(np.sum(xl[:, None, :] * gate.T[None, :, :], axis=-1))
    mix = np.sum(g.T[:, :, None] * z, axis=0)
    return x0 * (mix + b[None, :])


def reference(x0, xl, v, c, u, gate, b):
    R_out = core(x0, xl, v, c, u, gate, b)
    words, scales = planes(R_out.T)
    return R_out, words, scales

@@ -1,0 +1,596 @@
+from contextlib import ExitStack
+
+import concourse.mybir as mybir
+from concourse.masks import make_identity
+
+F32 = mybir.dt.float32
+BF16 = mybir.dt.bfloat16
+U32 = mybir.dt.uint32
+I32 = mybir.dt.int32
+U8 = mybir.dt.uint8
+FP8X4 = mybir.dt.float8_e4m3fn_x4
+ALU = mybir.AluOpType
+ACT = mybir.ActivationFunctionType
+AX = mybir.AxisListType
+
+N, D, R, E = 512, 1024, 512, 4
+P = 128
+SCM = (0, 2, 3)
+GB = 6
+CB = 3
+FLOPS = 2 * N * D * R * E * 2 + 2 * N * D * E
+
+
+def tile_dcnv2gatedlowrankcrossmixture_x1_kernel(tc, x0, xl, v, c, u, gate, b, out_0, out_1, out_2):
+    nc = tc.nc
+    with ExitStack() as ctx:
+        sb = ctx.enter_context(tc.tile_pool(name="sb", bufs=1))
+        ps = ctx.enter_context(tc.psum_pool(name="ps", bufs=4))
+        ctx.enter_context(tc.manual_schedule())
+
+        def one(shape, dtype, name):
+            return sb.tile(shape, dtype, name=name, tag=name, bufs=1, align_bytes=64)
+
+        ident = one([P, P], F32, "ident")
+        identb = one([P, P], BF16, "identb")
+        warm = one([P, 2], F32, "warm")
+        xraw = one([P, 4, D], BF16, "xraw")
+        xg = one([P, 2, N, 4], BF16, "xg")
+        xc = one([P, 2, N], U32, "xc")
+        xs = one([P, 2, N], U8, "xs")
+        gt = one([P, 2, 4, E], BF16, "gt")
+        ct = one([P, E, 4], BF16, "ct")
+        cf = one([P, E, 4], F32, "cf")
+        bb = one([P, D], BF16, "bb")
+        x0t = one([P, 4, D], BF16, "x0t")
+        acc = one([P, 4, D], F32, "acc")
+        yc = one([P, 2, N], U32, "yc")
+        ys = one([P, 2, N], U8, "ys")
+        mx = one([P, 4], F32, "mx")
+        dl = one([P, 4, E], F32, "dl")
+        ex = one([P, 4, E], F32, "ex")
+        sm = one([P, 4], F32, "sm")
+        rc = one([P, 4], F32, "rc")
+        gg = one([P, 4, E], F32, "gg")
+
+        vraw, uraw, grp, vcode, vscale, ucode, uscale = {}, {}, {}, {}, {}, {}, {}
+        pt, qb, qc, qs, zt, yb, yt, yg = {}, {}, {}, {}, {}, {}, {}, {}
+
+        def load_v(e, g):
+            if e not in vraw:
+                vraw[e] = sb.tile([P, 2, 4, R], BF16, name="vraw", tag="vraw", bufs=4, align_bytes=64)
+            nc.sync.dma_start(out=vraw[e][:, g, :, :], in_=v[e, 512 * g : 512 * g + 512, :].rearrange("(p j) r -> p j r", j=4))
+
+        def load_u(e):
+            uraw[e] = sb.tile([P, 4, D], BF16, name="uraw", tag="uraw", bufs=4, align_bytes=64)
+            nc.sync.dma_start(out=uraw[e][:], in_=u[e].rearrange("(p j) d -> p j d", j=4))
+
+        def load_x(t):
+            nc.sync.dma_start(out=xraw[:, t, :], in_=xl[P * t : P * t + P, :])
+
+        def copy_on(eng, dst, src):
+            if eng == "V":
+                nc.vector.tensor_copy(out=dst, in_=src)
+            else:
+                nc.scalar.copy(out=dst, in_=src)
+
+        def il_v(e, g, eng):
+            t_ = sb.tile([P, 2048], BF16, name="grp", tag="grp", bufs=GB, align_bytes=64)
+            grp["v", e, g] = t_
+            copy_on(
+                eng,
+                t_[:].rearrange("p (t m j) -> p m j t", t=4, j=4),
+                vraw[e][:, g, :, :].rearrange("p j (m t) -> p m j t", t=4),
+            )
+
+        def il_u(e, h, eng):
+            t_ = sb.tile([P, 2048], BF16, name="grp", tag="grp", bufs=GB, align_bytes=64)
+            grp["u", e, h] = t_
+            copy_on(
+                eng,
+                t_[:].rearrange("p (c i j) -> p c j i", i=4, j=4),
+                uraw[e][:, :, 512 * h : 512 * h + 512].rearrange("p j (c i) -> p c j i", i=4),
+            )
+
+        pb = {}
+
+        def pe_il(op, e, h, w):
+            if (op, e, h) not in grp:
+                grp[op, e, h] = sb.tile([P, 2048], BF16, name="grp", tag="grp", bufs=GB, align_bytes=64)
+            bank = ps.tile([P, 1024], BF16, name="pa", tag="pa", bufs=4)
+            pb[op, e, h, w] = bank
+            for y in range(2):
+                if op == "u":
+                    c0 = 512 * h + 256 * w + 128 * y
+                    rows = uraw[e][:, :, c0 : c0 + 128].rearrange("p j c -> p c j")
+                else:
+                    rows = vraw[e][:, h, :, 2 * w + y : R : 4].rearrange("p j m -> p m j")
+                nc.tensor.matmul(bank[:, 512 * y : 512 * y + 512], lhsT=identb[:], rhs=rows, start=True, stop=True)
+
+        def pe_cp(op, e, h, w, eng="S"):
+            copy_on(eng, grp[op, e, h][:, 1024 * w : 1024 * w + 1024], pb[op, e, h, w][:])
+
+        def il_pe(op, e, h):
+            for w in range(2):
+                pe_il(op, e, h, w)
+                pe_cp(op, e, h, w)
+
+        def q_v(e, g):
+            if e not in vcode:
+                vcode[e] = sb.tile([P, 2, R], U32, name="vcode", tag="vcode", bufs=CB, align_bytes=64)
+                vscale[e] = sb.tile([P, 2, R], U8, name="vscale", tag="vscale", bufs=CB, align_bytes=64)
+            nc.vector.quantize_mx(out=vcode[e][:, g, :].bitcast(FP8X4), scales=vscale[e][:, g, :], in_=grp["v", e, g][:])
+
+        def q_u(e, h):
+            if e not in ucode:
+                ucode[e] = sb.tile([P, 2, 512], U32, name="ucode", tag="ucode", bufs=CB, align_bytes=64)
+                uscale[e] = sb.tile([P, 2, 512], U8, name="uscale", tag="uscale", bufs=CB, align_bytes=64)
+            nc.vector.quantize_mx(out=ucode[e][:, h, :].bitcast(FP8X4), scales=uscale[e][:, h, :], in_=grp["u", e, h][:])
+
+        xps = {}
+
+        def tr_x(t):
+            xps[t] = ps.tile([P, 4, P], F32, name="pa", tag="pa", bufs=4)
+            words = xraw[:, t, :].bitcast(F32)
+            for g in range(2):
+                for w in range(2):
+                    nc.tensor.transpose(xps[t][:, 2 * g + w, :], words[:, 256 * g + w : 256 * g + 256 : 2], ident[:])
+
+        def cp_x(t, eng):
+            copy_on(
+                eng,
+                xg[:, :, P * t : P * t + P, :].bitcast(F32),
+                xps[t][:].rearrange("p (g w) r -> p g r w", g=2),
+            )
+
+        def q_x(g):
+            nc.vector.quantize_mx(
+                out=xc[:, g, :].bitcast(FP8X4), scales=xs[:, g, :], in_=xg[:, g, :, :].rearrange("p n j -> p (n j)")
+            )
+
+        lg = {}
+
+        def logits():
+            lg[0] = ps.tile([P, 4, E], F32, name="pz", tag="pz", bufs=4)
+            for t in range(4):
+                for k in range(8):
+                    nc.tensor.matmul(
+                        lg[0][:, t, :],
+                        lhsT=xg[:, k // 4, P * t : P * t + P, k % 4],
+                        rhs=gt[:, k // 4, k % 4, :],
+                        start=(k == 0),
+                        stop=(k == 7),
+                    )
+
+        def softmax(step):
+            if step == "sa":
+                nc.vector.reduce_max(out=mx[:], in_=lg[0][:], axis=AX.X)
+            elif step == "sb0":
+                nc.vector.tensor_tensor(out=dl[:], in0=lg[0][:], in1=mx[:].unsqueeze(2).to_broadcast([P, 4, E]), op=ALU.subtract)
+            elif step == "sb":
+                nc.scalar.activation(out=ex[:], in_=dl[:], func=ACT.Exp)
+            elif step == "sc0":
+                nc.vector.reduce_sum(out=sm[:], in_=ex[:], axis=AX.X)
+            elif step == "sc1":
+                nc.vector.reciprocal(out=rc[:], in_=sm[:])
+            else:
+                nc.vector.tensor_tensor(out=gg[:], in0=ex[:], in1=rc[:].unsqueeze(2).to_broadcast([P, 4, E]), op=ALU.mult)
+
+        def mm1(e, t):
+            a = ps.tile([P, N], F32, name="pa", tag="pa", bufs=4)
+            xps["m", e, t] = a
+            for g in range(2):
+                nc.tensor.matmul_mx(
+                    out=a[:],
+                    lhsT=vcode[e][:, g, P * t : P * t + P].bitcast(FP8X4),
+                    lhsT_scale=vscale[e][:, g, P * t : P * t + P],
+                    rhs=xc[:, g, :].bitcast(FP8X4),
+                    rhs_scale=xs[:, g, :],
+                    start=(g == 0),
+                    stop=(g == 1),
+                )
+
+        def tanh(e, t):
+            if e not in pt:
+                pt[e] = sb.tile([P, 4, N], F32, name="pt", tag="pt", bufs=2, align_bytes=64)
+            nc.scalar.activation(out=pt[e][:, t, :], in_=xps["m", e, t][:], func=ACT.Tanh)
+
+        def cmul(e, h):
+            if e not in qb:
+                qb[e] = sb.tile([P, N * 4], BF16, name="qb", tag="qb", bufs=2, align_bytes=64)
+            s = slice(256 * h, 256 * h + 256)
+            nc.vector.tensor_tensor(
+                out=qb[e][:, 1024 * h : 1024 * h + 1024].rearrange("p (c i t) -> p c t i", i=4, t=4),
+                in0=pt[e][:, :, s].rearrange("p t (c i) -> p c t i", i=4),
+                in1=ct[:, e, :].unsqueeze(1).unsqueeze(3).to_broadcast([P, 64, 4, 4]),
+                op=ALU.mult,
+            )
+
+        qt = {}
+
+        def cm_s(e, t):
+            if e not in qt:
+                qt[e] = sb.tile([P, 4, N], BF16, name="qt", tag="qt", bufs=2, align_bytes=64)
+            nc.scalar.activation(out=qt[e][:, t, :], in_=pt[e][:, t, :], func=ACT.Copy, scale=cf[:, e, t : t + 1])
+
+        def il_q(e, h):
+            if e not in qb:
+                qb[e] = sb.tile([P, N * 4], BF16, name="qb", tag="qb", bufs=2, align_bytes=64)
+            s = slice(256 * h, 256 * h + 256)
+            nc.vector.tensor_copy(
+                out=qb[e][:, 1024 * h : 1024 * h + 1024].rearrange("p (c i t) -> p c t i", i=4, t=4),
+                in_=qt[e][:, :, s].rearrange("p t (c i) -> p c t i", i=4),
+            )
+
+        def prod(e, h):
+            if e in SCM:
+                il_q(e, h)
+            else:
+                cmul(e, h)
+
+        def act(e):
+            for t in range(4):
+                mm1(e, t)
+                tanh(e, t)
+                if e in SCM and t > 0:
+                    cm_s(e, t - 1)
+            if e in SCM:
+                cm_s(e, 3)
+
+        def q_q(e, h):
+            if e not in qc:
+                qc[e] = sb.tile([P, N], U32, name="qc", tag="qc", bufs=4, align_bytes=64)
+                qs[e] = sb.tile([P, N], U8, name="qs", tag="qs", bufs=4, align_bytes=64)
+            s = slice(256 * h, 256 * h + 256)
+            nc.vector.quantize_mx(out=qc[e][:, s].bitcast(FP8X4), scales=qs[e][:, s], in_=qb[e][:, 1024 * h : 1024 * h + 1024])
+
+        def mm2(e, t, h):
+            z = ps.tile([P, 512], F32, name="pz", tag="pz", bufs=4)
+            zt[e, t, h] = z
+            nc.tensor.matmul_mx(
+                out=z[:],
+                lhsT=qc[e][:, P * t : P * t + P].bitcast(FP8X4),
+                lhsT_scale=qs[e][:, P * t : P * t + P],
+                rhs=ucode[e][:, h, :].bitcast(FP8X4),
+                rhs_scale=uscale[e][:, h, :],
+                start=True,
+                stop=True,
+            )
+
+        def mix(e, t, h):
+            s = slice(512 * h, 512 * h + 512)
+            nc.vector.scalar_tensor_tensor(
+                out=acc[:, t, s],
+                in0=zt[e, t, h][:],
+                scalar=gg[:, t, e : e + 1],
+                in1=bb[:, s] if e == 0 else acc[:, t, s],
+                op0=ALU.mult,
+                op1=ALU.add,
+            )
+
+        zg = {}
+
+        def scale_z(e, t, h):
+            zg[e, t, h] = sb.tile([P, 512], F32, name="zg", tag="zg", bufs=4, align_bytes=64)
+            nc.scalar.activation(out=zg[e, t, h][:], in_=zt[e, t, h][:], func=ACT.Copy, scale=gg[:, t, e : e + 1])
+
+        def add_z(e, t, h):
+            s = slice(512 * h, 512 * h + 512)
+            nc.gpsimd.tensor_tensor(
+                out=acc[:, t, s], in0=zg[e, t, h][:], in1=bb[:, s] if e == 0 else acc[:, t, s], op=ALU.add
+            )
+
+        def fin(t, h, eng=nc.vector):
+            s = slice(512 * h, 512 * h + 512)
+            eng.tensor_tensor(out=acc[:, t, s], in0=acc[:, t, s], in1=x0t[:, t, s], op=ALU.mult)
+
+        def st_o(t, h):
+            s = slice(512 * h, 512 * h + 512)
+            nc.sync.dma_start(out=out_0[P * t : P * t + P, s], in_=acc[:, t, s])
+
+        def cast_y(t, h):
+            if t not in yb:
+                yb[t] = sb.tile([P, D], BF16, name="yb", tag="yb", bufs=4, align_bytes=64)
+            s = slice(512 * h, 512 * h + 512)
+            nc.scalar.copy(out=yb[t][:, s], in_=acc[:, t, s])
+
+        def tr_y(t, h):
+            if t not in yt:
+                yt[t] = ps.tile([P, 4, P], F32, name="pa", tag="pa", bufs=4)
+            words = yb[t][:].bitcast(F32)
+            for w in range(2):
+                nc.tensor.transpose(yt[t][:, 2 * h + w, :], words[:, 256 * h + w : 256 * h + 256 : 2], ident[:])
+
+        def cp_y(t, eng):
+            yg[t] = sb.tile([P, 2, P, 4], BF16, name="yg", tag="yg", bufs=2, align_bytes=64)
+            copy_on(eng, yg[t][:].bitcast(F32), yt[t][:].rearrange("p (g w) r -> p g r w", g=2))
+
+        def q_y(t, h):
+            s = slice(P * t, P * t + P)
+            nc.vector.quantize_mx(
+                out=yc[:, h, s].bitcast(FP8X4), scales=ys[:, h, s], in_=yg[t][:, h, :, :].rearrange("p n j -> p (n j)")
+            )
+
+        def st_c(t):
+            nc.sync.dma_start(
+                out=out_1.bitcast(I32)[:, :, P * t : P * t + P, :].rearrange("g p m o -> p g (m o)"),
+                in_=yc[:, :, P * t : P * t + P].bitcast(I32),
+            )
+
+        def st_s(q):
+            nc.sync.dma_start(
+                out=out_2.bitcast(I32)[:, 4 * q : 4 * q + 4, :].rearrange("g q m -> q g m"),
+                in_=ys[32 * q : 32 * q + 4, :, :].bitcast(I32),
+            )
+
+        nc.vector.memset(warm[:], 0.0)
+        nc.scalar.activation(out=warm[:, 1:2], in_=warm[:, 0:1], func=ACT.Exp)
+        make_identity(nc, ident[:])
+        nc.gpsimd.tensor_copy(out=identb[:], in_=ident[:])
+        nc.gpsimd.dma_start(out=gt[:].rearrange("p g t e -> p g (t e)"), in_=gate.rearrange("(g p t) e -> p g (t e)", g=2, t=4))
+        nc.gpsimd.dma_start(out=ct[:], in_=c.rearrange("e (p t) -> p e t", t=4))
+        nc.gpsimd.tensor_copy(out=cf[:], in_=ct[:])
+        load_v(0, 0)
+        load_x(0)
+        load_x(1)
+        load_x(2)
+        load_x(3)
+        load_v(0, 1)
+        load_v(1, 0)
+        load_v(1, 1)
+        load_u(0)
+        nc.gpsimd.dma_start(out=bb[:], in_=b.partition_broadcast(P))
+        load_v(2, 0)
+        load_v(2, 1)
+        load_u(1)
+        load_v(3, 0)
+        load_v(3, 1)
+        load_u(2)
+        load_u(3)
+        nc.sync.dma_start(out=x0t[:], in_=x0.rearrange("(s p) d -> p s d", p=P))
+        il_v(0, 0, "S")
+        q_v(0, 0)
+        tr_x(0)
+        tr_x(1)
+        cp_x(1, "S")
+        tr_x(2)
+        cp_x(2, "S")
+        tr_x(3)
+        cp_x(0, "V")
+        cp_x(3, "V")
+        il_v(1, 0, "V")
+        q_x(0)
+        il_v(0, 1, "S")
+        q_v(0, 1)
+        logits()
+        q_x(1)
+        mm1(0, 3)
+        q_v(1, 0)
+        il_v(1, 1, "S")
+        il_u(0, 0, "V")
+        softmax("sa")
+        tanh(0, 3)
+        il_v(2, 0, "S")
+        cm_s(0, 3)
+        q_u(0, 0)
+        mm1(0, 2)
+        q_v(1, 1)
+        il_v(2, 1, "V")
+        softmax("sb0")
+        mm1(1, 3)
+        tanh(1, 3)
+        mm1(1, 1)
+        mm1(0, 0)
+        tanh(0, 2)
+        cm_s(0, 2)
+        q_v(2, 0)
+        tanh(0, 0)
+        tanh(1, 1)
+        cm_s(0, 0)
+        mm1(0, 1)
+        tanh(0, 1)
+        il_u(1, 0, "V")
+        cm_s(0, 1)
+        pe_il("u", 0, 1, 1)
+        pe_cp("u", 0, 1, 1)
+        softmax("sb")
+        pe_il("v", 3, 0, 1)
+        pe_cp("v", 3, 0, 1)
+        q_v(2, 1)
+        q_u(1, 0)
+        mm1(2, 3)
+        tanh(2, 3)
+        il_u(1, 1, "V")
+        il_v(3, 1, "V")
+        prod(0, 1)
+        prod(0, 0)
+        softmax("sc0")
+        q_q(0, 1)
+        mm1(1, 0)
+        pe_il("u", 0, 1, 0)
+        q_u(1, 1)
+        tanh(1, 0)
+        q_v(3, 1)
+        pe_il("v", 3, 0, 0)
+        pe_cp("u", 0, 1, 0)
+        mm1(1, 2)
+        softmax("sc1")
+        q_u(0, 1)
+        pe_cp("v", 3, 0, 0)
+        mm1(2, 0)
+        q_v(3, 0)
+        q_q(0, 0)
+        mm1(2, 1)
+        tanh(1, 2)
+        prod(1, 1)
+        prod(1, 0)
+        tanh(2, 0)
+        tanh(2, 1)
+        mm2(0, 2, 0)
+        cm_s(2, 1)
+        softmax("sc")
+        mm1(3, 1)
+        mm1(2, 2)
+        il_u(2, 0, "V")
+        mix(0, 2, 0)
+        mm2(0, 3, 0)
+        mix(0, 3, 0)
+        tanh(3, 1)
+        q_q(1, 1)
+        mm1(3, 2)
+        cm_s(2, 0)
+        tanh(3, 2)
+        pe_il("u", 3, 1, 1)
+        pe_cp("u", 3, 1, 1)
+        mm2(0, 1, 1)
+        mm2(0, 2, 1)
+        mix(0, 2, 1)
+        tanh(2, 2)
+        cm_s(2, 2)
+        pe_il("u", 3, 0, 1)
+        mm2(0, 1, 0)
+        mm1(3, 0)
+        mix(0, 1, 0)
+        mix(0, 1, 1)
+        cm_s(2, 3)
+        prod(2, 0)
+        prod(2, 1)
+        pe_cp("u", 3, 0, 1)
+        pe_il("u", 3, 1, 0)
+        mm2(1, 2, 1)
+        mix(1, 2, 1)
+        mm2(0, 0, 0)
+        cm_s(3, 2)
+        pe_cp("u", 3, 1, 0)
+        tanh(3, 0)
+        cm_s(3, 1)
+        scale_z(0, 0, 0)
+        q_q(1, 0)
+        cm_s(3, 0)
+        pe_il("u", 2, 1, 0)
+        q_u(2, 0)
+        mm1(3, 3)
+        mm2(0, 0, 1)
+        scale_z(0, 0, 1)
+        mm2(1, 3, 0)
+        mix(1, 3, 0)
+        add_z(0, 0, 1)
+        mm2(0, 3, 1)
+        mm2(1, 1, 0)
+        mix(1, 1, 0)
+        mix(0, 3, 1)
+        pe_il("u", 2, 1, 1)
+        mm2(1, 1, 1)
+        q_q(2, 0)
+        tanh(3, 3)
+        cm_s(3, 3)
+        prod(3, 0)
+        prod(3, 1)
+        pe_il("u", 3, 0, 0)
+        mix(1, 1, 1)
+        q_q(3, 0)
+        q_q(2, 1)
+        q_u(3, 1)
+        mm2(1, 0, 1)
+        pe_cp("u", 2, 1, 0)
+        pe_cp("u", 2, 1, 1)
+        scale_z(1, 0, 1)
+        add_z(0, 0, 0)
+        add_z(1, 0, 1)
+        q_u(2, 1)
+        mm2(1, 0, 0)
+        scale_z(1, 0, 0)
+        pe_cp("u", 3, 0, 0)
+        q_u(3, 0)
+        mm2(1, 2, 0)
+        mix(1, 2, 0)
+        mm2(2, 1, 0)
+        mix(2, 1, 0)
+        q_q(3, 1)
+        mm2(2, 0, 1)
+        scale_z(2, 0, 1)
+        add_z(1, 0, 0)
+        mm2(1, 3, 1)
+        mix(1, 3, 1)
+        mm2(3, 0, 1)
+        scale_z(3, 0, 1)
+        add_z(2, 0, 1)
+        mm2(2, 3, 0)
+        mix(2, 3, 0)
+        add_z(3, 0, 1)
+        mm2(2, 1, 1)
+        mix(2, 1, 1)
+        mm2(3, 1, 0)
+        mix(3, 1, 0)
+        mm2(2, 0, 0)
+        scale_z(2, 0, 0)
+        add_z(2, 0, 0)
+        mm2(2, 3, 1)
+        mix(2, 3, 1)
+        mm2(2, 2, 0)
+        mix(2, 2, 0)
+        mm2(3, 1, 1)
+        mix(3, 1, 1)
+        mm2(3, 3, 0)
+        mm2(2, 2, 1)
+        mix(2, 2, 1)
+        fin(1, 0, nc.gpsimd)
+        st_o(1, 0)
+        cast_y(1, 0)
+        mix(3, 3, 0)
+        mm2(3, 3, 1)
+        mm2(3, 0, 0)
+        fin(0, 1, nc.gpsimd)
+        st_o(0, 1)
+        mm2(3, 2, 0)
+        mix(3, 3, 1)
+        mix(3, 2, 0)
+        fin(3, 1)
+        st_o(3, 1)
+        scale_z(3, 0, 0)
+        mm2(3, 2, 1)
+        mix(3, 2, 1)
+        fin(3, 0)
+        st_o(3, 0)
+        cast_y(0, 1)
+        fin(2, 0)
+        st_o(2, 0)
+        cast_y(3, 1)
+        fin(1, 1, nc.gpsimd)
+        st_o(1, 1)
+        add_z(3, 0, 0)
+        cast_y(1, 1)
+        tr_y(1, 0)
+        tr_y(1, 1)
+        cast_y(3, 0)
+        tr_y(3, 0)
+        tr_y(3, 1)
+        fin(0, 0, nc.gpsimd)
+        st_o(0, 0)
+        cast_y(2, 0)
+        fin(2, 1)
+        st_o(2, 1)
+        cast_y(2, 1)
+        cast_y(0, 0)
+        tr_y(2, 0)
+        tr_y(2, 1)
+        cp_y(1, "V")
+        q_y(1, 0)
+        q_y(1, 1)
+        st_c(1)
+        cp_y(3, "V")
+        q_y(3, 0)
+        q_y(3, 1)
+        st_c(3)
+        cp_y(2, "S")
+        q_y(2, 1)
+        q_y(2, 0)
+        st_c(2)
+        tr_y(0, 0)
+        tr_y(0, 1)
+        cp_y(0, "S")
+        q_y(0, 1)
+        q_y(0, 0)
+        st_c(0)
+        for q in range(4):
+            st_s(q)

@@ -15,9 +15,9 @@ AX = mybir.AxisListType
 
 N, D, R, E = 512, 1024, 512, 4
 P = 128
-SCM = (0, 2, 3)
+SCM = (2, 3)
 GB = 6
-CB = 3
+CB = 4
 FLOPS = 2 * N * D * R * E * 2 + 2 * N * D * E
 
 
@@ -34,15 +34,14 @@ def tile_dcnv2gatedlowrankcrossmixture_x1_kernel(tc, x0, xl, v, c, u, gate, b, o
         ident = one([P, P], F32, "ident")
         identb = one([P, P], BF16, "identb")
         warm = one([P, 2], F32, "warm")
-        xraw = one([P, 4, D], BF16, "xraw")
+        xraw = sb.tile([P, 4, D], BF16, name="xraw", tag="xrow", bufs=1, align_bytes=64)
         xg = one([P, 2, N, 4], BF16, "xg")
         xc = one([P, 2, N], U32, "xc")
         xs = one([P, 2, N], U8, "xs")
         gt = one([P, 2, 4, E], BF16, "gt")
-        ct = one([P, E, 4], BF16, "ct")
+        crow = one([P, R], BF16, "crow")
         cf = one([P, E, 4], F32, "cf")
         bb = one([P, D], BF16, "bb")
-        x0t = one([P, 4, D], BF16, "x0t")
         acc = one([P, 4, D], F32, "acc")
         yc = one([P, 2, N], U32, "yc")
         ys = one([P, 2, N], U8, "ys")
@@ -202,7 +201,7 @@ def tile_dcnv2gatedlowrankcrossmixture_x1_kernel(tc, x0, xl, v, c, u, gate, b, o
             nc.vector.tensor_tensor(
                 out=qb[e][:, 1024 * h : 1024 * h + 1024].rearrange("p (c i t) -> p c t i", i=4, t=4),
                 in0=pt[e][:, :, s].rearrange("p t (c i) -> p c t i", i=4),
-                in1=ct[:, e, :].unsqueeze(1).unsqueeze(3).to_broadcast([P, 64, 4, 4]),
+                in1=cf[:, e, :].unsqueeze(1).unsqueeze(3).to_broadcast([P, 64, 4, 4]),
                 op=ALU.mult,
             )
 
@@ -323,274 +322,272 @@ def tile_dcnv2gatedlowrankcrossmixture_x1_kernel(tc, x0, xl, v, c, u, gate, b, o
                 in_=ys[32 * q : 32 * q + 4, :, :].bitcast(I32),
             )
 
+        def c_columns():
+            bank = ps.tile([P, 4, P], BF16, name="pz", tag="pz", bufs=4)
+            for t in range(4):
+                nc.tensor.transpose(bank[:, t, :], crow[:, t : R : 4], identb[:])
+            nc.vector.tensor_copy(out=cf[:].rearrange("p e t -> p t e"), in_=bank[:, :, 0:E])
+
         nc.vector.memset(warm[:], 0.0)
+        nc.vector.memset(crow[:], 0.0)
         nc.scalar.activation(out=warm[:, 1:2], in_=warm[:, 0:1], func=ACT.Exp)
         make_identity(nc, ident[:])
         nc.gpsimd.tensor_copy(out=identb[:], in_=ident[:])
-        nc.gpsimd.dma_start(out=gt[:].rearrange("p g t e -> p g (t e)"), in_=gate.rearrange("(g p t) e -> p g (t e)", g=2, t=4))
-        nc.gpsimd.dma_start(out=ct[:], in_=c.rearrange("e (p t) -> p e t", t=4))
-        nc.gpsimd.tensor_copy(out=cf[:], in_=ct[:])
-        load_v(0, 0)
+        nc.scalar.dma_start(out=crow[0:E, :], in_=c)
         load_x(0)
         load_x(1)
+        load_v(0, 0)
         load_x(2)
         load_x(3)
         load_v(0, 1)
+        nc.sync.dma_start(out=gt[:].rearrange("p g t e -> p g (t e)"), in_=gate.rearrange("(g p t) e -> p g (t e)", g=2, t=4))
         load_v(1, 0)
         load_v(1, 1)
         load_u(0)
-        nc.gpsimd.dma_start(out=bb[:], in_=b.partition_broadcast(P))
+        load_u(1)
         load_v(2, 0)
         load_v(2, 1)
-        load_u(1)
+        load_u(2)
         load_v(3, 0)
         load_v(3, 1)
-        load_u(2)
+        nc.sync.dma_start(out=bb[:], in_=b.partition_broadcast(P))
         load_u(3)
-        nc.sync.dma_start(out=x0t[:], in_=x0.rearrange("(s p) d -> p s d", p=P))
-        il_v(0, 0, "S")
-        q_v(0, 0)
+        il_v(0, 0, "V")
         tr_x(0)
+        cp_x(0, "V")
         tr_x(1)
-        cp_x(1, "S")
+        cp_x(1, "V")
         tr_x(2)
         cp_x(2, "S")
         tr_x(3)
-        cp_x(0, "V")
-        cp_x(3, "V")
-        il_v(1, 0, "V")
-        q_x(0)
-        il_v(0, 1, "S")
+        il_v(0, 1, "V")
         q_v(0, 1)
-        logits()
+        q_v(0, 0)
+        cp_x(3, "S")
         q_x(1)
+        c_columns()
+        logits()
+        x0t = sb.tile([P, 4, D], BF16, name="x0t", tag="xrow", bufs=1, align_bytes=64)
+        nc.sync.dma_start(out=x0t[:], in_=x0.rearrange("(s p) d -> p s d", p=P))
+        q_x(0)
+        mm1(0, 1)
         mm1(0, 3)
+        il_v(1, 0, "S")
         q_v(1, 0)
         il_v(1, 1, "S")
         il_u(0, 0, "V")
-        softmax("sa")
-        tanh(0, 3)
-        il_v(2, 0, "S")
-        cm_s(0, 3)
         q_u(0, 0)
-        mm1(0, 2)
-        q_v(1, 1)
-        il_v(2, 1, "V")
-        softmax("sb0")
-        mm1(1, 3)
-        tanh(1, 3)
-        mm1(1, 1)
         mm1(0, 0)
-        tanh(0, 2)
-        cm_s(0, 2)
-        q_v(2, 0)
-        tanh(0, 0)
-        tanh(1, 1)
-        cm_s(0, 0)
-        mm1(0, 1)
-        tanh(0, 1)
+        q_v(1, 1)
+        mm1(1, 1)
         il_u(1, 0, "V")
-        cm_s(0, 1)
-        pe_il("u", 0, 1, 1)
-        pe_cp("u", 0, 1, 1)
-        softmax("sb")
-        pe_il("v", 3, 0, 1)
-        pe_cp("v", 3, 0, 1)
-        q_v(2, 1)
+        il_u(0, 1, "S")
+        softmax("sa")
         q_u(1, 0)
-        mm1(2, 3)
-        tanh(2, 3)
-        il_u(1, 1, "V")
-        il_v(3, 1, "V")
-        prod(0, 1)
-        prod(0, 0)
-        softmax("sc0")
-        q_q(0, 1)
-        mm1(1, 0)
-        pe_il("u", 0, 1, 0)
-        q_u(1, 1)
-        tanh(1, 0)
-        q_v(3, 1)
-        pe_il("v", 3, 0, 0)
-        pe_cp("u", 0, 1, 0)
-        mm1(1, 2)
-        softmax("sc1")
+        tanh(0, 1)
+        softmax("sb0")
+        tanh(1, 1)
         q_u(0, 1)
-        pe_cp("v", 3, 0, 0)
+        tanh(0, 3)
+        mm1(0, 2)
+        tanh(0, 2)
+        il_v(2, 1, "V")
+        tanh(0, 0)
+        il_u(1, 1, "V")
+        prod(0, 1)
+        q_v(2, 1)
+        pe_il("v", 2, 0, 1)
+        il_u(2, 1, "S")
+        prod(0, 0)
+        q_u(2, 1)
+        pe_il("v", 2, 0, 0)
+        il_v(3, 0, "V")
+        mm1(1, 2)
+        pe_cp("v", 2, 0, 1)
+        pe_cp("v", 2, 0, 0)
+        q_q(0, 1)
+        mm1(1, 3)
+        pe_il("u", 2, 0, 1)
+        tanh(1, 2)
+        mm1(1, 0)
+        q_u(1, 1)
+        q_v(2, 0)
+        softmax("sb")
+        softmax("sc0")
+        pe_il("v", 3, 1, 0)
+        tanh(1, 3)
+        tanh(1, 0)
+        prod(1, 1)
+        mm2(0, 2, 0)
+        prod(1, 0)
+        pe_cp("v", 3, 1, 0)
+        pe_il("v", 3, 1, 1)
+        softmax("sc1")
+        q_q(0, 0)
+        softmax("sc")
+        pe_cp("u", 2, 0, 1)
+        il_u(3, 0, "V")
+        mm1(2, 3)
         mm1(2, 0)
         q_v(3, 0)
-        q_q(0, 0)
-        mm1(2, 1)
-        tanh(1, 2)
-        prod(1, 1)
-        prod(1, 0)
-        tanh(2, 0)
-        tanh(2, 1)
-        mm2(0, 2, 0)
-        cm_s(2, 1)
-        softmax("sc")
-        mm1(3, 1)
-        mm1(2, 2)
-        il_u(2, 0, "V")
-        mix(0, 2, 0)
-        mm2(0, 3, 0)
-        mix(0, 3, 0)
-        tanh(3, 1)
+        il_u(3, 1, "S")
         q_q(1, 1)
-        mm1(3, 2)
-        cm_s(2, 0)
-        tanh(3, 2)
-        pe_il("u", 3, 1, 1)
-        pe_cp("u", 3, 1, 1)
-        mm2(0, 1, 1)
-        mm2(0, 2, 1)
-        mix(0, 2, 1)
-        tanh(2, 2)
-        cm_s(2, 2)
-        pe_il("u", 3, 0, 1)
-        mm2(0, 1, 0)
-        mm1(3, 0)
-        mix(0, 1, 0)
-        mix(0, 1, 1)
-        cm_s(2, 3)
-        prod(2, 0)
-        prod(2, 1)
-        pe_cp("u", 3, 0, 1)
-        pe_il("u", 3, 1, 0)
-        mm2(1, 2, 1)
-        mix(1, 2, 1)
+        pe_cp("v", 3, 1, 1)
+        mix(0, 2, 0)
+        mm1(2, 2)
         mm2(0, 0, 0)
-        cm_s(3, 2)
-        pe_cp("u", 3, 1, 0)
-        tanh(3, 0)
-        cm_s(3, 1)
-        scale_z(0, 0, 0)
+        tanh(2, 3)
+        tanh(2, 0)
+        mm2(0, 3, 0)
         q_q(1, 0)
-        cm_s(3, 0)
-        pe_il("u", 2, 1, 0)
-        q_u(2, 0)
+        mm1(2, 1)
+        tanh(2, 1)
+        cm_s(2, 0)
+        pe_il("u", 2, 0, 0)
+        pe_cp("u", 2, 0, 0)
+        mix(0, 3, 0)
+        mm2(0, 1, 0)
+        q_v(3, 1)
+        q_u(3, 1)
+        cm_s(2, 1)
+        tanh(2, 2)
+        mm1(3, 1)
+        mm2(0, 2, 1)
+        cm_s(2, 3)
+        q_u(3, 0)
         mm1(3, 3)
-        mm2(0, 0, 1)
-        scale_z(0, 0, 1)
+        q_u(2, 0)
+        scale_z(0, 0, 0)
+        cm_s(2, 2)
+        mix(0, 1, 0)
         mm2(1, 3, 0)
         mix(1, 3, 0)
-        add_z(0, 0, 1)
-        mm2(0, 3, 1)
-        mm2(1, 1, 0)
-        mix(1, 1, 0)
-        mix(0, 3, 1)
-        pe_il("u", 2, 1, 1)
-        mm2(1, 1, 1)
-        q_q(2, 0)
+        add_z(0, 0, 0)
+        mm2(0, 0, 1)
+        mm1(3, 0)
+        tanh(3, 0)
+        prod(2, 1)
+        mix(0, 2, 1)
         tanh(3, 3)
         cm_s(3, 3)
-        prod(3, 0)
-        prod(3, 1)
-        pe_il("u", 3, 0, 0)
-        mix(1, 1, 1)
-        q_q(3, 0)
         q_q(2, 1)
-        q_u(3, 1)
-        mm2(1, 0, 1)
-        pe_cp("u", 2, 1, 0)
-        pe_cp("u", 2, 1, 1)
-        scale_z(1, 0, 1)
-        add_z(0, 0, 0)
-        add_z(1, 0, 1)
-        q_u(2, 1)
-        mm2(1, 0, 0)
-        scale_z(1, 0, 0)
-        pe_cp("u", 3, 0, 0)
-        q_u(3, 0)
+        prod(2, 0)
+        tanh(3, 1)
         mm2(1, 2, 0)
+        mm1(3, 2)
+        mm2(1, 2, 1)
         mix(1, 2, 0)
-        mm2(2, 1, 0)
-        mix(2, 1, 0)
-        q_q(3, 1)
-        mm2(2, 0, 1)
-        scale_z(2, 0, 1)
-        add_z(1, 0, 0)
-        mm2(1, 3, 1)
-        mix(1, 3, 1)
-        mm2(3, 0, 1)
-        scale_z(3, 0, 1)
-        add_z(2, 0, 1)
+        mix(1, 2, 1)
+        scale_z(0, 0, 1)
+        add_z(0, 0, 1)
         mm2(2, 3, 0)
         mix(2, 3, 0)
-        add_z(3, 0, 1)
-        mm2(2, 1, 1)
-        mix(2, 1, 1)
-        mm2(3, 1, 0)
-        mix(3, 1, 0)
+        mm2(1, 0, 1)
+        mm2(0, 3, 1)
+        mix(0, 3, 1)
+        mm2(1, 1, 0)
+        cm_s(3, 0)
+        scale_z(1, 0, 1)
+        mm2(0, 1, 1)
+        tanh(3, 2)
+        cm_s(3, 1)
+        mix(0, 1, 1)
+        mix(1, 1, 0)
+        q_q(2, 0)
+        mm2(1, 1, 1)
+        mix(1, 1, 1)
+        add_z(1, 0, 1)
+        mm2(1, 3, 1)
+        mix(1, 3, 1)
+        mm2(1, 0, 0)
+        cm_s(3, 2)
+        mm2(2, 2, 1)
+        prod(3, 1)
+        mix(2, 2, 1)
+        scale_z(1, 0, 0)
+        add_z(1, 0, 0)
         mm2(2, 0, 0)
         scale_z(2, 0, 0)
-        add_z(2, 0, 0)
-        mm2(2, 3, 1)
-        mix(2, 3, 1)
-        mm2(2, 2, 0)
-        mix(2, 2, 0)
-        mm2(3, 1, 1)
-        mix(3, 1, 1)
+        mm2(2, 0, 1)
+        q_q(3, 1)
+        scale_z(2, 0, 1)
+        prod(3, 0)
         mm2(3, 3, 0)
-        mm2(2, 2, 1)
-        mix(2, 2, 1)
-        fin(1, 0, nc.gpsimd)
-        st_o(1, 0)
-        cast_y(1, 0)
         mix(3, 3, 0)
-        mm2(3, 3, 1)
-        mm2(3, 0, 0)
-        fin(0, 1, nc.gpsimd)
-        st_o(0, 1)
-        mm2(3, 2, 0)
-        mix(3, 3, 1)
-        mix(3, 2, 0)
-        fin(3, 1)
-        st_o(3, 1)
-        scale_z(3, 0, 0)
+        q_q(3, 0)
         mm2(3, 2, 1)
         mix(3, 2, 1)
+        mm2(3, 0, 0)
         fin(3, 0)
         st_o(3, 0)
-        cast_y(0, 1)
-        fin(2, 0)
-        st_o(2, 0)
-        cast_y(3, 1)
-        fin(1, 1, nc.gpsimd)
-        st_o(1, 1)
-        add_z(3, 0, 0)
-        cast_y(1, 1)
-        tr_y(1, 0)
-        tr_y(1, 1)
-        cast_y(3, 0)
-        tr_y(3, 0)
-        tr_y(3, 1)
-        fin(0, 0, nc.gpsimd)
-        st_o(0, 0)
-        cast_y(2, 0)
+        add_z(2, 0, 1)
+        add_z(2, 0, 0)
+        scale_z(3, 0, 0)
+        mm2(2, 2, 0)
+        mix(2, 2, 0)
+        mm2(3, 0, 1)
+        scale_z(3, 0, 1)
+        mm2(3, 2, 0)
+        mm2(3, 3, 1)
         fin(2, 1)
         st_o(2, 1)
+        cast_y(3, 0)
         cast_y(2, 1)
+        mm2(2, 3, 1)
+        mix(3, 2, 0)
+        add_z(3, 0, 0)
+        mix(2, 3, 1)
+        mm2(2, 1, 0)
+        mix(2, 1, 0)
+        mm2(2, 1, 1)
+        fin(2, 0)
+        st_o(2, 0)
+        cast_y(2, 0)
+        mix(3, 3, 1)
+        mix(2, 1, 1)
+        fin(3, 1)
+        st_o(3, 1)
+        add_z(3, 0, 1)
+        cast_y(3, 1)
+        mm2(3, 1, 0)
+        fin(0, 0, nc.gpsimd)
+        st_o(0, 0)
+        mm2(3, 1, 1)
         cast_y(0, 0)
+        mix(3, 1, 0)
+        fin(0, 1, nc.gpsimd)
+        st_o(0, 1)
         tr_y(2, 0)
         tr_y(2, 1)
-        cp_y(1, "V")
-        q_y(1, 0)
-        q_y(1, 1)
-        st_c(1)
-        cp_y(3, "V")
-        q_y(3, 0)
-        q_y(3, 1)
-        st_c(3)
-        cp_y(2, "S")
-        q_y(2, 1)
+        tr_y(3, 0)
+        tr_y(3, 1)
+        mix(3, 1, 1)
+        cast_y(0, 1)
+        fin(1, 0)
+        st_o(1, 0)
+        cast_y(1, 0)
+        fin(1, 1)
+        st_o(1, 1)
+        cast_y(1, 1)
+        cp_y(2, "V")
         q_y(2, 0)
-        st_c(2)
         tr_y(0, 0)
         tr_y(0, 1)
+        q_y(2, 1)
+        st_c(2)
+        tr_y(1, 0)
+        tr_y(1, 1)
+        cp_y(3, "S")
+        q_y(3, 1)
+        q_y(3, 0)
+        st_c(3)
         cp_y(0, "S")
         q_y(0, 1)
         q_y(0, 0)
         st_c(0)
+        cp_y(1, "S")
+        q_y(1, 0)
+        q_y(1, 1)
+        st_c(1)
         for q in range(4):
             st_s(q)

@@ -78,8 +78,8 @@ def tile_dcnv2gatedlowrankcrossmixture_x1_kernel(tc, x0, xl, v, c, u, gate, b, o
             grp["v", e, g] = t_
             copy_on(
                 eng,
-                t_[:].rearrange("p (t m j) -> p m j t", t=4, j=4),
-                vraw[e][:, g, :, :].rearrange("p j (m t) -> p m j t", t=4),
+                t_[:].rearrange("p (t m j) -> p m t j", t=4, j=4),
+                vraw[e][:, g, :, :].rearrange("p j (m t) -> p m t j", t=4),
             )
 
         def il_u(e, h, eng):

@@ -15,9 +15,8 @@ AX = mybir.AxisListType
 
 N, D, R, E = 512, 1024, 512, 4
 P = 128
-SCM = (2, 3)
-GB = 6
-CB = 4
+SCM = (1, 2, 3)
+GB, CB, PB, RAW = 4, 4, 2, 4
 FLOPS = 2 * N * D * R * E * 2 + 2 * N * D * E
 
 
@@ -28,41 +27,54 @@ def tile_dcnv2gatedlowrankcrossmixture_x1_kernel(tc, x0, xl, v, c, u, gate, b, o
         ps = ctx.enter_context(tc.psum_pool(name="ps", bufs=4))
         ctx.enter_context(tc.manual_schedule())
 
-        def one(shape, dtype, name):
-            return sb.tile(shape, dtype, name=name, tag=name, bufs=1, align_bytes=64)
+        def keep(shape, dtype, name, bufs=1):
+            return sb.tile(shape, dtype, name=name, tag=name, bufs=bufs, align_bytes=64)
 
-        ident = one([P, P], F32, "ident")
-        identb = one([P, P], BF16, "identb")
-        warm = one([P, 2], F32, "warm")
-        xraw = sb.tile([P, 4, D], BF16, name="xraw", tag="xrow", bufs=1, align_bytes=64)
-        xg = one([P, 2, N, 4], BF16, "xg")
-        xc = one([P, 2, N], U32, "xc")
-        xs = one([P, 2, N], U8, "xs")
-        gt = one([P, 2, 4, E], BF16, "gt")
-        crow = one([P, R], BF16, "crow")
-        cf = one([P, E, 4], F32, "cf")
-        bb = one([P, D], BF16, "bb")
-        acc = one([P, 4, D], F32, "acc")
-        yc = one([P, 2, N], U32, "yc")
-        ys = one([P, 2, N], U8, "ys")
-        mx = one([P, 4], F32, "mx")
-        dl = one([P, 4, E], F32, "dl")
-        ex = one([P, 4, E], F32, "ex")
-        sm = one([P, 4], F32, "sm")
-        rc = one([P, 4], F32, "rc")
-        gg = one([P, 4, E], F32, "gg")
+        ident = keep([P, P], F32, "ident")
+        identb = keep([P, P], BF16, "identb")
+        warm = keep([P, 2], F32, "warm")
+        xraw = keep([P, 4, D], BF16, "rows")
+        xg = keep([P, 2, N, 4], BF16, "xg")
+        xc = keep([P, 2, N], U32, "xc")
+        xs = keep([P, 2, N], U8, "xs")
+        gt = keep([P, 2, 4, E], BF16, "gt")
+        crow = keep([P, R], BF16, "crow")
+        cf = keep([P, E, 4], F32, "cf")
+        bb = keep([P, D], BF16, "bb")
+        acc = keep([P, 4, D], F32, "acc")
+        yc = keep([P, 2, N], U32, "yc")
+        ys = keep([P, 2, N], U8, "ys")
+        mx = keep([P, 4], F32, "mx")
+        dl = keep([P, 4, E], F32, "dl")
+        ex = keep([P, 4, E], F32, "ex")
+        sm = keep([P, 4], F32, "sm")
+        rc = keep([P, 4], F32, "rc")
+        gg = keep([P, 4, E], F32, "gg")
 
-        vraw, uraw, grp, vcode, vscale, ucode, uscale = {}, {}, {}, {}, {}, {}, {}
-        pt, qb, qc, qs, zt, yb, yt, yg = {}, {}, {}, {}, {}, {}, {}, {}
+        vraw, uraw, grp, codes, scales, bank = {}, {}, {}, {}, {}, {}
+        pt, qt, qb, zg, yb, yg = {}, {}, {}, {}, {}, {}
+
+        def tile_of(tiles, key, shape, dtype, name, bufs):
+            if key not in tiles:
+                tiles[key] = sb.tile(shape, dtype, name=name, tag=name, bufs=bufs, align_bytes=64)
+            return tiles[key]
+
+        def psum(key, shape, dtype, name):
+            bank[key] = ps.tile(shape, dtype, name=name, tag=name, bufs=4)
+            return bank[key]
 
         def load_v(e, g):
-            if e not in vraw:
-                vraw[e] = sb.tile([P, 2, 4, R], BF16, name="vraw", tag="vraw", bufs=4, align_bytes=64)
-            nc.sync.dma_start(out=vraw[e][:, g, :, :], in_=v[e, 512 * g : 512 * g + 512, :].rearrange("(p j) r -> p j r", j=4))
+            t_ = tile_of(vraw, e, [P, 2, 4, R], BF16, "vraw", RAW)
+            if e == 0:
+                nc.sync.dma_start(out=t_[:, g, :, :], in_=v[e, 512 * g : 512 * g + 512, :].rearrange("(p j) r -> p j r", j=4))
+            elif g == 0:
+                nc.sync.dma_start(
+                    out=t_[:].rearrange("p g j r -> p g (j r)"), in_=v[e].rearrange("(g p j) r -> p g (j r)", g=2, j=4)
+                )
 
         def load_u(e):
-            uraw[e] = sb.tile([P, 4, D], BF16, name="uraw", tag="uraw", bufs=4, align_bytes=64)
-            nc.sync.dma_start(out=uraw[e][:], in_=u[e].rearrange("(p j) d -> p j d", j=4))
+            t_ = tile_of(uraw, e, [P, 4, D], BF16, "uraw", RAW)
+            nc.sync.dma_start(out=t_[:], in_=u[e].rearrange("(p j) d -> p j d", j=4))
 
         def load_x(t):
             nc.sync.dma_start(out=xraw[:, t, :], in_=xl[P * t : P * t + P, :])
@@ -73,99 +85,87 @@ def tile_dcnv2gatedlowrankcrossmixture_x1_kernel(tc, x0, xl, v, c, u, gate, b, o
             else:
                 nc.scalar.copy(out=dst, in_=src)
 
+        def grouped(op, e):
+            return tile_of(grp, (op, e), [P, 4096], BF16, "grp", GB)
+
         def il_v(e, g, eng):
-            t_ = sb.tile([P, 2048], BF16, name="grp", tag="grp", bufs=GB, align_bytes=64)
-            grp["v", e, g] = t_
             copy_on(
                 eng,
-                t_[:].rearrange("p (t m j) -> p m t j", t=4, j=4),
+                grouped("v", e)[:, 2048 * g : 2048 * g + 2048].rearrange("p (t m j) -> p m t j", t=4, j=4),
                 vraw[e][:, g, :, :].rearrange("p j (m t) -> p m t j", t=4),
             )
 
         def il_u(e, h, eng):
-            t_ = sb.tile([P, 2048], BF16, name="grp", tag="grp", bufs=GB, align_bytes=64)
-            grp["u", e, h] = t_
             copy_on(
                 eng,
-                t_[:].rearrange("p (c i j) -> p c j i", i=4, j=4),
+                grouped("u", e)[:, 2048 * h : 2048 * h + 2048].rearrange("p (c i j) -> p c j i", i=4, j=4),
                 uraw[e][:, :, 512 * h : 512 * h + 512].rearrange("p j (c i) -> p c j i", i=4),
             )
 
-        pb = {}
-
         def pe_il(op, e, h, w):
-            if (op, e, h) not in grp:
-                grp[op, e, h] = sb.tile([P, 2048], BF16, name="grp", tag="grp", bufs=GB, align_bytes=64)
-            bank = ps.tile([P, 1024], BF16, name="pa", tag="pa", bufs=4)
-            pb[op, e, h, w] = bank
+            out = psum((op, e, h, w), [P, 1024], BF16, "pa")
             for y in range(2):
                 if op == "u":
                     c0 = 512 * h + 256 * w + 128 * y
                     rows = uraw[e][:, :, c0 : c0 + 128].rearrange("p j c -> p c j")
                 else:
                     rows = vraw[e][:, h, :, 2 * w + y : R : 4].rearrange("p j m -> p m j")
-                nc.tensor.matmul(bank[:, 512 * y : 512 * y + 512], lhsT=identb[:], rhs=rows, start=True, stop=True)
+                nc.tensor.matmul(out[:, 512 * y : 512 * y + 512], lhsT=identb[:], rhs=rows, start=True, stop=True)
 
-        def pe_cp(op, e, h, w, eng="S"):
-            copy_on(eng, grp[op, e, h][:, 1024 * w : 1024 * w + 1024], pb[op, e, h, w][:])
+        def pe_cp(op, e, h, w):
+            c0 = 2048 * h + 1024 * w
+            nc.scalar.copy(out=grouped(op, e)[:, c0 : c0 + 1024], in_=bank[op, e, h, w][:])
 
-        def il_pe(op, e, h):
-            for w in range(2):
-                pe_il(op, e, h, w)
-                pe_cp(op, e, h, w)
+        def quantize(key, width, src, bufs):
+            k = tile_of(codes, key, [P, width], U32, "c" + key[0], bufs)
+            s = tile_of(scales, key, [P, width], U8, "s" + key[0], bufs)
+            nc.vector.quantize_mx(out=k[:].bitcast(FP8X4), scales=s[:], in_=src)
 
-        def q_v(e, g):
-            if e not in vcode:
-                vcode[e] = sb.tile([P, 2, R], U32, name="vcode", tag="vcode", bufs=CB, align_bytes=64)
-                vscale[e] = sb.tile([P, 2, R], U8, name="vscale", tag="vscale", bufs=CB, align_bytes=64)
-            nc.vector.quantize_mx(out=vcode[e][:, g, :].bitcast(FP8X4), scales=vscale[e][:, g, :], in_=grp["v", e, g][:])
-
-        def q_u(e, h):
-            if e not in ucode:
-                ucode[e] = sb.tile([P, 2, 512], U32, name="ucode", tag="ucode", bufs=CB, align_bytes=64)
-                uscale[e] = sb.tile([P, 2, 512], U8, name="uscale", tag="uscale", bufs=CB, align_bytes=64)
-            nc.vector.quantize_mx(out=ucode[e][:, h, :].bitcast(FP8X4), scales=uscale[e][:, h, :], in_=grp["u", e, h][:])
-
-        xps = {}
+        def q_w(op, e):
+            quantize((op, e), 1024, grp[op, e][:], 3 if op == "v" else 4)
 
         def tr_x(t):
-            xps[t] = ps.tile([P, 4, P], F32, name="pa", tag="pa", bufs=4)
+            out = psum(("x", t), [P, 4, P], F32, "pa")
             words = xraw[:, t, :].bitcast(F32)
             for g in range(2):
                 for w in range(2):
-                    nc.tensor.transpose(xps[t][:, 2 * g + w, :], words[:, 256 * g + w : 256 * g + 256 : 2], ident[:])
+                    nc.tensor.transpose(out[:, 2 * g + w, :], words[:, 256 * g + w : 256 * g + 256 : 2], ident[:])
 
         def cp_x(t, eng):
-            copy_on(
-                eng,
-                xg[:, :, P * t : P * t + P, :].bitcast(F32),
-                xps[t][:].rearrange("p (g w) r -> p g r w", g=2),
-            )
+            copy_on(eng, xg[:, :, P * t : P * t + P, :].bitcast(F32), bank["x", t][:].rearrange("p (g w) r -> p g r w", g=2))
 
-        def q_x(g):
+        def q_x():
             nc.vector.quantize_mx(
-                out=xc[:, g, :].bitcast(FP8X4), scales=xs[:, g, :], in_=xg[:, g, :, :].rearrange("p n j -> p (n j)")
+                out=xc[:].rearrange("p g n -> p (g n)").bitcast(FP8X4),
+                scales=xs[:].rearrange("p g n -> p (g n)"),
+                in_=xg[:].rearrange("p g n j -> p (g n j)"),
             )
-
-        lg = {}
 
         def logits():
-            lg[0] = ps.tile([P, 4, E], F32, name="pz", tag="pz", bufs=4)
+            out = psum("l", [P, 4, E], F32, "pz")
             for t in range(4):
                 for k in range(8):
                     nc.tensor.matmul(
-                        lg[0][:, t, :],
+                        out[:, t, :],
                         lhsT=xg[:, k // 4, P * t : P * t + P, k % 4],
                         rhs=gt[:, k // 4, k % 4, :],
                         start=(k == 0),
                         stop=(k == 7),
                     )
 
+        def c_columns():
+            out = psum("c", [P, 4, P], BF16, "pz")
+            for t in range(4):
+                nc.tensor.transpose(out[:, t, :], crow[:, t : R : 4], identb[:])
+            nc.vector.tensor_copy(out=cf[:].rearrange("p e t -> p t e"), in_=out[:, :, 0:E])
+
         def softmax(step):
             if step == "sa":
-                nc.vector.reduce_max(out=mx[:], in_=lg[0][:], axis=AX.X)
+                nc.vector.reduce_max(out=mx[:], in_=bank["l"][:], axis=AX.X)
             elif step == "sb0":
-                nc.vector.tensor_tensor(out=dl[:], in0=lg[0][:], in1=mx[:].unsqueeze(2).to_broadcast([P, 4, E]), op=ALU.subtract)
+                nc.vector.tensor_tensor(
+                    out=dl[:], in0=bank["l"][:], in1=mx[:].unsqueeze(2).to_broadcast([P, 4, E]), op=ALU.subtract
+                )
             elif step == "sb":
                 nc.scalar.activation(out=ex[:], in_=dl[:], func=ACT.Exp)
             elif step == "sc0":
@@ -176,13 +176,13 @@ def tile_dcnv2gatedlowrankcrossmixture_x1_kernel(tc, x0, xl, v, c, u, gate, b, o
                 nc.vector.tensor_tensor(out=gg[:], in0=ex[:], in1=rc[:].unsqueeze(2).to_broadcast([P, 4, E]), op=ALU.mult)
 
         def mm1(e, t):
-            a = ps.tile([P, N], F32, name="pa", tag="pa", bufs=4)
-            xps["m", e, t] = a
+            out = psum(("p", e, t), [P, N], F32, "pa")
             for g in range(2):
+                s = slice(R * g + P * t, R * g + P * t + P)
                 nc.tensor.matmul_mx(
-                    out=a[:],
-                    lhsT=vcode[e][:, g, P * t : P * t + P].bitcast(FP8X4),
-                    lhsT_scale=vscale[e][:, g, P * t : P * t + P],
+                    out=out[:],
+                    lhsT=codes["v", e][:, s].bitcast(FP8X4),
+                    lhsT_scale=scales["v", e][:, s],
                     rhs=xc[:, g, :].bitcast(FP8X4),
                     rhs_scale=xs[:, g, :],
                     start=(g == 0),
@@ -190,143 +190,104 @@ def tile_dcnv2gatedlowrankcrossmixture_x1_kernel(tc, x0, xl, v, c, u, gate, b, o
                 )
 
         def tanh(e, t):
-            if e not in pt:
-                pt[e] = sb.tile([P, 4, N], F32, name="pt", tag="pt", bufs=2, align_bytes=64)
-            nc.scalar.activation(out=pt[e][:, t, :], in_=xps["m", e, t][:], func=ACT.Tanh)
-
-        def cmul(e, h):
-            if e not in qb:
-                qb[e] = sb.tile([P, N * 4], BF16, name="qb", tag="qb", bufs=2, align_bytes=64)
-            s = slice(256 * h, 256 * h + 256)
-            nc.vector.tensor_tensor(
-                out=qb[e][:, 1024 * h : 1024 * h + 1024].rearrange("p (c i t) -> p c t i", i=4, t=4),
-                in0=pt[e][:, :, s].rearrange("p t (c i) -> p c t i", i=4),
-                in1=cf[:, e, :].unsqueeze(1).unsqueeze(3).to_broadcast([P, 64, 4, 4]),
-                op=ALU.mult,
-            )
-
-        qt = {}
+            out = tile_of(pt, e, [P, 4, N], F32, "pt", PB)
+            nc.scalar.activation(out=out[:, t, :], in_=bank["p", e, t][:], func=ACT.Tanh)
 
         def cm_s(e, t):
-            if e not in qt:
-                qt[e] = sb.tile([P, 4, N], BF16, name="qt", tag="qt", bufs=2, align_bytes=64)
-            nc.scalar.activation(out=qt[e][:, t, :], in_=pt[e][:, t, :], func=ACT.Copy, scale=cf[:, e, t : t + 1])
+            out = tile_of(qt, e, [P, 4, N], BF16, "qt", 2)
+            nc.scalar.activation(out=out[:, t, :], in_=pt[e][:, t, :], func=ACT.Copy, scale=cf[:, e, t : t + 1])
 
-        def il_q(e, h):
-            if e not in qb:
-                qb[e] = sb.tile([P, N * 4], BF16, name="qb", tag="qb", bufs=2, align_bytes=64)
-            s = slice(256 * h, 256 * h + 256)
-            nc.vector.tensor_copy(
-                out=qb[e][:, 1024 * h : 1024 * h + 1024].rearrange("p (c i t) -> p c t i", i=4, t=4),
-                in_=qt[e][:, :, s].rearrange("p t (c i) -> p c t i", i=4),
-            )
-
-        def prod(e, h):
+        def prod(e):
+            out = tile_of(qb, e, [P, N * 4], BF16, "qb", 2)
             if e in SCM:
-                il_q(e, h)
+                nc.vector.tensor_copy(
+                    out=out[:].rearrange("p (c i t) -> p c t i", i=4, t=4), in_=qt[e][:].rearrange("p t (c i) -> p c t i", i=4)
+                )
             else:
-                cmul(e, h)
+                nc.vector.tensor_tensor(
+                    out=out[:].rearrange("p (c i t) -> p c t i", i=2, t=4),
+                    in0=pt[e][:].rearrange("p t (c i) -> p c t i", i=2),
+                    in1=cf[:, e, :].unsqueeze(1).unsqueeze(3).to_broadcast([P, 256, 4, 2]),
+                    op=ALU.mult,
+                )
 
-        def act(e):
-            for t in range(4):
-                mm1(e, t)
-                tanh(e, t)
-                if e in SCM and t > 0:
-                    cm_s(e, t - 1)
-            if e in SCM:
-                cm_s(e, 3)
-
-        def q_q(e, h):
-            if e not in qc:
-                qc[e] = sb.tile([P, N], U32, name="qc", tag="qc", bufs=4, align_bytes=64)
-                qs[e] = sb.tile([P, N], U8, name="qs", tag="qs", bufs=4, align_bytes=64)
-            s = slice(256 * h, 256 * h + 256)
-            nc.vector.quantize_mx(out=qc[e][:, s].bitcast(FP8X4), scales=qs[e][:, s], in_=qb[e][:, 1024 * h : 1024 * h + 1024])
+        def q_q(e):
+            quantize(("q", e), N, qb[e][:], 4)
 
         def mm2(e, t, h):
-            z = ps.tile([P, 512], F32, name="pz", tag="pz", bufs=4)
-            zt[e, t, h] = z
+            out = psum(("z", e, t, h), [P, 512], F32, "pz")
+            rows = slice(P * t, P * t + P)
+            cols = slice(512 * h, 512 * h + 512)
             nc.tensor.matmul_mx(
-                out=z[:],
-                lhsT=qc[e][:, P * t : P * t + P].bitcast(FP8X4),
-                lhsT_scale=qs[e][:, P * t : P * t + P],
-                rhs=ucode[e][:, h, :].bitcast(FP8X4),
-                rhs_scale=uscale[e][:, h, :],
+                out=out[:],
+                lhsT=codes["q", e][:, rows].bitcast(FP8X4),
+                lhsT_scale=scales["q", e][:, rows],
+                rhs=codes["u", e][:, cols].bitcast(FP8X4),
+                rhs_scale=scales["u", e][:, cols],
                 start=True,
                 stop=True,
             )
 
-        def mix(e, t, h):
+        def before(e, t, h):
             s = slice(512 * h, 512 * h + 512)
+            return bb[:, s] if e == 0 else acc[:, t, s]
+
+        def mix(e, t, h):
             nc.vector.scalar_tensor_tensor(
-                out=acc[:, t, s],
-                in0=zt[e, t, h][:],
+                out=acc[:, t, 512 * h : 512 * h + 512],
+                in0=bank["z", e, t, h][:],
                 scalar=gg[:, t, e : e + 1],
-                in1=bb[:, s] if e == 0 else acc[:, t, s],
+                in1=before(e, t, h),
                 op0=ALU.mult,
                 op1=ALU.add,
             )
 
-        zg = {}
-
         def scale_z(e, t, h):
-            zg[e, t, h] = sb.tile([P, 512], F32, name="zg", tag="zg", bufs=4, align_bytes=64)
-            nc.scalar.activation(out=zg[e, t, h][:], in_=zt[e, t, h][:], func=ACT.Copy, scale=gg[:, t, e : e + 1])
+            out = tile_of(zg, (e, t, h), [P, 512], F32, "zg", 3)
+            nc.scalar.activation(out=out[:], in_=bank["z", e, t, h][:], func=ACT.Copy, scale=gg[:, t, e : e + 1])
 
         def add_z(e, t, h):
-            s = slice(512 * h, 512 * h + 512)
-            nc.gpsimd.tensor_tensor(
-                out=acc[:, t, s], in0=zg[e, t, h][:], in1=bb[:, s] if e == 0 else acc[:, t, s], op=ALU.add
-            )
+            nc.gpsimd.tensor_tensor(out=acc[:, t, 512 * h : 512 * h + 512], in0=zg[e, t, h][:], in1=before(e, t, h), op=ALU.add)
 
         def fin(t, h, eng=nc.vector):
             s = slice(512 * h, 512 * h + 512)
             eng.tensor_tensor(out=acc[:, t, s], in0=acc[:, t, s], in1=x0t[:, t, s], op=ALU.mult)
-
-        def st_o(t, h):
-            s = slice(512 * h, 512 * h + 512)
             nc.sync.dma_start(out=out_0[P * t : P * t + P, s], in_=acc[:, t, s])
 
         def cast_y(t, h):
-            if t not in yb:
-                yb[t] = sb.tile([P, D], BF16, name="yb", tag="yb", bufs=4, align_bytes=64)
             s = slice(512 * h, 512 * h + 512)
-            nc.scalar.copy(out=yb[t][:, s], in_=acc[:, t, s])
+            nc.scalar.copy(out=tile_of(yb, t, [P, D], BF16, "yb", 4)[:, s], in_=acc[:, t, s])
 
-        def tr_y(t, h):
-            if t not in yt:
-                yt[t] = ps.tile([P, 4, P], F32, name="pa", tag="pa", bufs=4)
+        def tr_y(t):
+            out = psum(("y", t), [P, 4, P], F32, "pa")
             words = yb[t][:].bitcast(F32)
-            for w in range(2):
-                nc.tensor.transpose(yt[t][:, 2 * h + w, :], words[:, 256 * h + w : 256 * h + 256 : 2], ident[:])
+            for g in range(2):
+                for w in range(2):
+                    nc.tensor.transpose(out[:, 2 * g + w, :], words[:, 256 * g + w : 256 * g + 256 : 2], ident[:])
 
         def cp_y(t, eng):
-            yg[t] = sb.tile([P, 2, P, 4], BF16, name="yg", tag="yg", bufs=2, align_bytes=64)
-            copy_on(eng, yg[t][:].bitcast(F32), yt[t][:].rearrange("p (g w) r -> p g r w", g=2))
+            out = tile_of(yg, t, [P, 2, P, 4], BF16, "yg", 2)
+            copy_on(eng, out[:].bitcast(F32), bank["y", t][:].rearrange("p (g w) r -> p g r w", g=2))
 
-        def q_y(t, h):
+        def q_y(t):
             s = slice(P * t, P * t + P)
-            nc.vector.quantize_mx(
-                out=yc[:, h, s].bitcast(FP8X4), scales=ys[:, h, s], in_=yg[t][:, h, :, :].rearrange("p n j -> p (n j)")
-            )
-
-        def st_c(t):
+            for g in range(2):
+                nc.vector.quantize_mx(
+                    out=yc[:, g, s].bitcast(FP8X4),
+                    scales=ys[:, g, s],
+                    in_=yg[t][:, g, :, :].rearrange("p n j -> p (n j)"),
+                )
             nc.sync.dma_start(
-                out=out_1.bitcast(I32)[:, :, P * t : P * t + P, :].rearrange("g p m o -> p g (m o)"),
-                in_=yc[:, :, P * t : P * t + P].bitcast(I32),
+                out=out_1.bitcast(I32)[:, :, s, :].rearrange("g p m o -> p g (m o)"), in_=yc[:, :, s].bitcast(I32)
             )
 
-        def st_s(q):
-            nc.sync.dma_start(
-                out=out_2.bitcast(I32)[:, 4 * q : 4 * q + 4, :].rearrange("g q m -> q g m"),
-                in_=ys[32 * q : 32 * q + 4, :, :].bitcast(I32),
-            )
-
-        def c_columns():
-            bank = ps.tile([P, 4, P], BF16, name="pz", tag="pz", bufs=4)
-            for t in range(4):
-                nc.tensor.transpose(bank[:, t, :], crow[:, t : R : 4], identb[:])
-            nc.vector.tensor_copy(out=cf[:].rearrange("p e t -> p t e"), in_=bank[:, :, 0:E])
+        def store_scales():
+            for q in range(4):
+                queue = (nc.sync, nc.scalar)[q % 2]
+                queue.dma_start(
+                    out=out_2.bitcast(I32)[:, 4 * q : 4 * q + 4, :].rearrange("g q m -> q g m"),
+                    in_=ys[32 * q : 32 * q + 4, :, :].bitcast(I32),
+                )
 
         nc.vector.memset(warm[:], 0.0)
         nc.vector.memset(crow[:], 0.0)
@@ -342,252 +303,210 @@ def tile_dcnv2gatedlowrankcrossmixture_x1_kernel(tc, x0, xl, v, c, u, gate, b, o
         load_v(0, 1)
         nc.sync.dma_start(out=gt[:].rearrange("p g t e -> p g (t e)"), in_=gate.rearrange("(g p t) e -> p g (t e)", g=2, t=4))
         load_v(1, 0)
-        load_v(1, 1)
         load_u(0)
         load_u(1)
         load_v(2, 0)
-        load_v(2, 1)
         load_u(2)
         load_v(3, 0)
-        load_v(3, 1)
         nc.sync.dma_start(out=bb[:], in_=b.partition_broadcast(P))
         load_u(3)
-        il_v(0, 0, "V")
         tr_x(0)
-        cp_x(0, "V")
+        il_v(0, 0, "V")
+        cp_x(0, "S")
         tr_x(1)
-        cp_x(1, "V")
+        cp_x(1, "S")
         tr_x(2)
         cp_x(2, "S")
-        tr_x(3)
         il_v(0, 1, "V")
-        q_v(0, 1)
-        q_v(0, 0)
+        tr_x(3)
+        x0t = keep([P, 4, D], BF16, "rows")
+        nc.sync.dma_start(out=x0t[:], in_=x0.rearrange("(s p) d -> p s d", p=P))
         cp_x(3, "S")
-        q_x(1)
+        q_x()
         c_columns()
         logits()
-        x0t = sb.tile([P, 4, D], BF16, name="x0t", tag="xrow", bufs=1, align_bytes=64)
-        nc.sync.dma_start(out=x0t[:], in_=x0.rearrange("(s p) d -> p s d", p=P))
-        q_x(0)
-        mm1(0, 1)
-        mm1(0, 3)
-        il_v(1, 0, "S")
-        q_v(1, 0)
+        q_w("v", 0)
         il_v(1, 1, "S")
-        il_u(0, 0, "V")
-        q_u(0, 0)
-        mm1(0, 0)
-        q_v(1, 1)
-        mm1(1, 1)
-        il_u(1, 0, "V")
         il_u(0, 1, "S")
+        il_v(1, 0, "V")
+        il_u(0, 0, "V")
+        mm1(0, 1)
+        q_w("v", 1)
         softmax("sa")
-        q_u(1, 0)
         tanh(0, 1)
-        softmax("sb0")
-        tanh(1, 1)
-        q_u(0, 1)
+        mm1(0, 3)
         tanh(0, 3)
         mm1(0, 2)
-        tanh(0, 2)
-        il_v(2, 1, "V")
-        tanh(0, 0)
         il_u(1, 1, "V")
-        prod(0, 1)
-        q_v(2, 1)
-        pe_il("v", 2, 0, 1)
-        il_u(2, 1, "S")
-        prod(0, 0)
-        q_u(2, 1)
-        pe_il("v", 2, 0, 0)
-        il_v(3, 0, "V")
-        mm1(1, 2)
-        pe_cp("v", 2, 0, 1)
-        pe_cp("v", 2, 0, 0)
-        q_q(0, 1)
+        tanh(0, 2)
+        mm1(0, 0)
+        tanh(0, 0)
         mm1(1, 3)
-        pe_il("u", 2, 0, 1)
-        tanh(1, 2)
-        mm1(1, 0)
-        q_u(1, 1)
-        q_v(2, 0)
-        softmax("sb")
-        softmax("sc0")
-        pe_il("v", 3, 1, 0)
         tanh(1, 3)
-        tanh(1, 0)
-        prod(1, 1)
-        mm2(0, 2, 0)
-        prod(1, 0)
-        pe_cp("v", 3, 1, 0)
-        pe_il("v", 3, 1, 1)
-        softmax("sc1")
-        q_q(0, 0)
-        softmax("sc")
-        pe_cp("u", 2, 0, 1)
-        il_u(3, 0, "V")
-        mm1(2, 3)
-        mm1(2, 0)
-        q_v(3, 0)
-        il_u(3, 1, "S")
-        q_q(1, 1)
-        pe_cp("v", 3, 1, 1)
-        mix(0, 2, 0)
-        mm1(2, 2)
+        cm_s(1, 3)
+        q_w("u", 0)
+        softmax("sb0")
+        softmax("sb")
+        mm1(1, 1)
+        tanh(1, 1)
+        mm1(1, 2)
+        tanh(1, 2)
+        cm_s(1, 1)
+        pe_il("v", 2, 1, 1)
+        pe_il("v", 2, 1, 0)
+        pe_cp("v", 2, 1, 1)
+        prod(0)
+        il_v(2, 0, "V")
+        softmax("sc0")
+        q_q(0)
         mm2(0, 0, 0)
-        tanh(2, 3)
-        tanh(2, 0)
+        pe_cp("v", 2, 1, 0)
+        pe_il("v", 3, 0, 0)
+        softmax("sc1")
+        il_u(1, 0, "S")
+        il_v(3, 1, "V")
+        mm1(1, 0)
+        cm_s(1, 2)
+        q_w("v", 2)
+        softmax("sc")
+        q_w("u", 1)
+        pe_il("v", 3, 0, 1)
+        mm2(0, 1, 0)
+        pe_cp("v", 3, 0, 0)
         mm2(0, 3, 0)
-        q_q(1, 0)
+        mm2(0, 0, 1)
+        mix(0, 0, 0)
+        il_u(2, 0, "V")
+        pe_cp("v", 3, 0, 1)
+        tanh(1, 0)
+        cm_s(1, 0)
+        prod(1)
+        mix(0, 1, 0)
+        mm2(0, 1, 1)
+        mm1(2, 2)
+        tanh(2, 2)
+        pe_il("u", 2, 1, 1)
+        pe_cp("u", 2, 1, 1)
         mm1(2, 1)
         tanh(2, 1)
-        cm_s(2, 0)
-        pe_il("u", 2, 0, 0)
-        pe_cp("u", 2, 0, 0)
-        mix(0, 3, 0)
-        mm2(0, 1, 0)
-        q_v(3, 1)
-        q_u(3, 1)
         cm_s(2, 1)
-        tanh(2, 2)
-        mm1(3, 1)
-        mm2(0, 2, 1)
+        q_q(1)
+        mm1(2, 3)
+        tanh(2, 3)
         cm_s(2, 3)
-        q_u(3, 0)
-        mm1(3, 3)
-        q_u(2, 0)
-        scale_z(0, 0, 0)
         cm_s(2, 2)
-        mix(0, 1, 0)
+        q_w("v", 3)
+        mm2(0, 2, 1)
+        mix(0, 3, 0)
+        pe_il("u", 2, 1, 0)
+        pe_cp("u", 2, 1, 0)
+        mm1(2, 0)
+        mm2(1, 0, 1)
+        mm1(3, 2)
+        tanh(3, 2)
+        mix(0, 1, 1)
+        mix(0, 0, 1)
+        mm1(3, 1)
+        mix(0, 2, 1)
+        mix(1, 0, 1)
+        il_u(3, 0, "S")
+        mm1(3, 0)
+        q_w("u", 2)
+        mm2(1, 1, 0)
+        tanh(2, 0)
         mm2(1, 3, 0)
         mix(1, 3, 0)
-        add_z(0, 0, 0)
-        mm2(0, 0, 1)
-        mm1(3, 0)
-        tanh(3, 0)
-        prod(2, 1)
-        mix(0, 2, 1)
-        tanh(3, 3)
-        cm_s(3, 3)
-        q_q(2, 1)
-        prod(2, 0)
-        tanh(3, 1)
-        mm2(1, 2, 0)
-        mm1(3, 2)
-        mm2(1, 2, 1)
-        mix(1, 2, 0)
-        mix(1, 2, 1)
-        scale_z(0, 0, 1)
-        add_z(0, 0, 1)
-        mm2(2, 3, 0)
-        mix(2, 3, 0)
-        mm2(1, 0, 1)
         mm2(0, 3, 1)
-        mix(0, 3, 1)
-        mm2(1, 1, 0)
-        cm_s(3, 0)
-        scale_z(1, 0, 1)
-        mm2(0, 1, 1)
-        tanh(3, 2)
-        cm_s(3, 1)
-        mix(0, 1, 1)
         mix(1, 1, 0)
-        q_q(2, 0)
         mm2(1, 1, 1)
         mix(1, 1, 1)
-        add_z(1, 0, 1)
+        mm2(0, 2, 0)
+        cm_s(2, 0)
         mm2(1, 3, 1)
+        tanh(3, 0)
+        cm_s(3, 0)
+        mix(0, 3, 1)
+        pe_il("u", 3, 1, 0)
+        prod(2)
         mix(1, 3, 1)
-        mm2(1, 0, 0)
-        cm_s(3, 2)
-        mm2(2, 2, 1)
-        prod(3, 1)
-        mix(2, 2, 1)
-        scale_z(1, 0, 0)
-        add_z(1, 0, 0)
-        mm2(2, 0, 0)
-        scale_z(2, 0, 0)
+        mm1(3, 3)
+        tanh(3, 3)
+        pe_cp("u", 3, 1, 0)
+        tanh(3, 1)
+        q_q(2)
+        mm2(2, 3, 1)
+        cm_s(3, 3)
+        mix(0, 2, 0)
+        mix(2, 3, 1)
         mm2(2, 0, 1)
-        q_q(3, 1)
-        scale_z(2, 0, 1)
-        prod(3, 0)
+        cm_s(3, 2)
+        mm2(2, 3, 0)
+        mix(2, 0, 1)
+        mm2(1, 2, 0)
+        mm2(2, 1, 0)
+        mm2(2, 1, 1)
+        mix(2, 3, 0)
+        pe_il("u", 3, 1, 1)
+        cm_s(3, 1)
+        mix(2, 1, 0)
+        mix(1, 2, 0)
+        prod(3)
+        pe_cp("u", 3, 1, 1)
+        q_w("u", 3)
+        q_q(3)
+        mm2(1, 0, 0)
+        mix(1, 0, 0)
+        mm2(3, 1, 0)
+        mm2(3, 0, 1)
+        mix(2, 1, 1)
         mm2(3, 3, 0)
+        mix(3, 1, 0)
+        mix(3, 0, 1)
         mix(3, 3, 0)
-        q_q(3, 0)
-        mm2(3, 2, 1)
-        mix(3, 2, 1)
-        mm2(3, 0, 0)
+        fin(1, 0)
+        mm2(3, 3, 1)
+        mix(3, 3, 1)
+        mm2(2, 0, 0)
+        cast_y(1, 0)
+        mm2(3, 1, 1)
+        mix(3, 1, 1)
+        fin(0, 1)
+        mm2(1, 2, 1)
+        mix(1, 2, 1)
         fin(3, 0)
-        st_o(3, 0)
-        add_z(2, 0, 1)
-        add_z(2, 0, 0)
-        scale_z(3, 0, 0)
+        mm2(2, 2, 1)
+        cast_y(0, 1)
+        fin(1, 1)
+        cast_y(1, 1)
+        mix(2, 0, 0)
+        fin(3, 1)
+        cast_y(3, 1)
+        cast_y(3, 0)
+        mix(2, 2, 1)
+        mm2(3, 0, 0)
+        mix(3, 0, 0)
         mm2(2, 2, 0)
         mix(2, 2, 0)
-        mm2(3, 0, 1)
-        scale_z(3, 0, 1)
+        tr_y(1)
+        fin(0, 0)
         mm2(3, 2, 0)
-        mm2(3, 3, 1)
-        fin(2, 1)
-        st_o(2, 1)
-        cast_y(3, 0)
-        cast_y(2, 1)
-        mm2(2, 3, 1)
-        mix(3, 2, 0)
-        add_z(3, 0, 0)
-        mix(2, 3, 1)
-        mm2(2, 1, 0)
-        mix(2, 1, 0)
-        mm2(2, 1, 1)
-        fin(2, 0)
-        st_o(2, 0)
-        cast_y(2, 0)
-        mix(3, 3, 1)
-        mix(2, 1, 1)
-        fin(3, 1)
-        st_o(3, 1)
-        add_z(3, 0, 1)
-        cast_y(3, 1)
-        mm2(3, 1, 0)
-        fin(0, 0, nc.gpsimd)
-        st_o(0, 0)
-        mm2(3, 1, 1)
-        cast_y(0, 0)
-        mix(3, 1, 0)
-        fin(0, 1, nc.gpsimd)
-        st_o(0, 1)
-        tr_y(2, 0)
-        tr_y(2, 1)
-        tr_y(3, 0)
-        tr_y(3, 1)
-        mix(3, 1, 1)
-        cast_y(0, 1)
-        fin(1, 0)
-        st_o(1, 0)
-        cast_y(1, 0)
-        fin(1, 1)
-        st_o(1, 1)
-        cast_y(1, 1)
-        cp_y(2, "V")
-        q_y(2, 0)
-        tr_y(0, 0)
-        tr_y(0, 1)
-        q_y(2, 1)
-        st_c(2)
-        tr_y(1, 0)
-        tr_y(1, 1)
-        cp_y(3, "S")
-        q_y(3, 1)
-        q_y(3, 0)
-        st_c(3)
-        cp_y(0, "S")
-        q_y(0, 1)
-        q_y(0, 0)
-        st_c(0)
         cp_y(1, "S")
-        q_y(1, 0)
-        q_y(1, 1)
-        st_c(1)
-        for q in range(4):
-            st_s(q)
+        cast_y(0, 0)
+        mm2(3, 2, 1)
+        tr_y(3)
+        mix(3, 2, 0)
+        tr_y(0)
+        cp_y(3, "S")
+        mix(3, 2, 1)
+        fin(2, 0)
+        fin(2, 1)
+        q_y(1)
+        cp_y(0, "V")
+        cast_y(2, 0)
+        q_y(3)
+        q_y(0)
+        cast_y(2, 1)
+        tr_y(2)
+        cp_y(2, "S")
+        q_y(2)
+        store_scales()

from contextlib import ExitStack

import concourse.mybir as mybir
from concourse.masks import make_identity

F32 = mybir.dt.float32
BF16 = mybir.dt.bfloat16
U32 = mybir.dt.uint32
I32 = mybir.dt.int32
U8 = mybir.dt.uint8
FP8X4 = mybir.dt.float8_e4m3fn_x4
ALU = mybir.AluOpType
ACT = mybir.ActivationFunctionType
AX = mybir.AxisListType

N, D, R, E = 512, 1024, 512, 4
P = 128
SCM = (1, 2, 3)
GB, CB, PB, RAW = 4, 4, 2, 4
FLOPS = 2 * N * D * R * E * 2 + 2 * N * D * E


def tile_dcnv2gatedlowrankcrossmixture_x1_kernel(tc, x0, xl, v, c, u, gate, b, out_0, out_1, out_2):
    nc = tc.nc
    with ExitStack() as ctx:
        sb = ctx.enter_context(tc.tile_pool(name="sb", bufs=1))
        ps = ctx.enter_context(tc.psum_pool(name="ps", bufs=4))
        ctx.enter_context(tc.manual_schedule())

        def keep(shape, dtype, name, bufs=1):
            return sb.tile(shape, dtype, name=name, tag=name, bufs=bufs, align_bytes=64)

        ident = keep([P, P], F32, "ident")
        identb = keep([P, P], BF16, "identb")
        warm = keep([P, 2], F32, "warm")
        xraw = keep([P, 4, D], BF16, "rows")
        xg = keep([P, 2, N, 4], BF16, "xg")
        xc = keep([P, 2, N], U32, "xc")
        xs = keep([P, 2, N], U8, "xs")
        gt = keep([P, 2, 4, E], BF16, "gt")
        crow = keep([P, R], BF16, "crow")
        cf = keep([P, E, 4], F32, "cf")
        bb = keep([P, D], BF16, "bb")
        acc = keep([P, 4, D], F32, "acc")
        yc = keep([P, 2, N], U32, "yc")
        ys = keep([P, 2, N], U8, "ys")
        mx = keep([P, 4], F32, "mx")
        dl = keep([P, 4, E], F32, "dl")
        ex = keep([P, 4, E], F32, "ex")
        sm = keep([P, 4], F32, "sm")
        rc = keep([P, 4], F32, "rc")
        gg = keep([P, 4, E], F32, "gg")

        vraw, uraw, grp, codes, scales, bank = {}, {}, {}, {}, {}, {}
        pt, qt, qb, zg, yb, yg = {}, {}, {}, {}, {}, {}

        def tile_of(tiles, key, shape, dtype, name, bufs):
            if key not in tiles:
                tiles[key] = sb.tile(shape, dtype, name=name, tag=name, bufs=bufs, align_bytes=64)
            return tiles[key]

        def psum(key, shape, dtype, name):
            bank[key] = ps.tile(shape, dtype, name=name, tag=name, bufs=4)
            return bank[key]

        def load_v(e, g):
            t_ = tile_of(vraw, e, [P, 2, 4, R], BF16, "vraw", RAW)
            if e == 0:
                nc.sync.dma_start(out=t_[:, g, :, :], in_=v[e, 512 * g : 512 * g + 512, :].rearrange("(p j) r -> p j r", j=4))
            elif g == 0:
                nc.sync.dma_start(
                    out=t_[:].rearrange("p g j r -> p g (j r)"), in_=v[e].rearrange("(g p j) r -> p g (j r)", g=2, j=4)
                )

        def load_u(e):
            t_ = tile_of(uraw, e, [P, 4, D], BF16, "uraw", RAW)
            nc.sync.dma_start(out=t_[:], in_=u[e].rearrange("(p j) d -> p j d", j=4))

        def load_x(t):
            nc.sync.dma_start(out=xraw[:, t, :], in_=xl[P * t : P * t + P, :])

        def copy_on(eng, dst, src):
            if eng == "V":
                nc.vector.tensor_copy(out=dst, in_=src)
            else:
                nc.scalar.copy(out=dst, in_=src)

        def grouped(op, e):
            return tile_of(grp, (op, e), [P, 4096], BF16, "grp", GB)

        def il_v(e, g, eng):
            copy_on(
                eng,
                grouped("v", e)[:, 2048 * g : 2048 * g + 2048].rearrange("p (t m j) -> p m t j", t=4, j=4),
                vraw[e][:, g, :, :].rearrange("p j (m t) -> p m t j", t=4),
            )

        def il_u(e, h, eng):
            copy_on(
                eng,
                grouped("u", e)[:, 2048 * h : 2048 * h + 2048].rearrange("p (c i j) -> p c j i", i=4, j=4),
                uraw[e][:, :, 512 * h : 512 * h + 512].rearrange("p j (c i) -> p c j i", i=4),
            )

        def pe_il(op, e, h, w):
            out = psum((op, e, h, w), [P, 1024], BF16, "pa")
            for y in range(2):
                if op == "u":
                    c0 = 512 * h + 256 * w + 128 * y
                    rows = uraw[e][:, :, c0 : c0 + 128].rearrange("p j c -> p c j")
                else:
                    rows = vraw[e][:, h, :, 2 * w + y : R : 4].rearrange("p j m -> p m j")
                nc.tensor.matmul(out[:, 512 * y : 512 * y + 512], lhsT=identb[:], rhs=rows, start=True, stop=True)

        def pe_cp(op, e, h, w):
            c0 = 2048 * h + 1024 * w
            nc.scalar.copy(out=grouped(op, e)[:, c0 : c0 + 1024], in_=bank[op, e, h, w][:])

        def quantize(key, width, src, bufs):
            k = tile_of(codes, key, [P, width], U32, "c" + key[0], bufs)
            s = tile_of(scales, key, [P, width], U8, "s" + key[0], bufs)
            nc.vector.quantize_mx(out=k[:].bitcast(FP8X4), scales=s[:], in_=src)

        def q_w(op, e):
            quantize((op, e), 1024, grp[op, e][:], 3 if op == "v" else 4)

        def tr_x(t):
            out = psum(("x", t), [P, 4, P], F32, "pa")
            words = xraw[:, t, :].bitcast(F32)
            for g in range(2):
                for w in range(2):
                    nc.tensor.transpose(out[:, 2 * g + w, :], words[:, 256 * g + w : 256 * g + 256 : 2], ident[:])

        def cp_x(t, eng):
            copy_on(eng, xg[:, :, P * t : P * t + P, :].bitcast(F32), bank["x", t][:].rearrange("p (g w) r -> p g r w", g=2))

        def q_x():
            nc.vector.quantize_mx(
                out=xc[:].rearrange("p g n -> p (g n)").bitcast(FP8X4),
                scales=xs[:].rearrange("p g n -> p (g n)"),
                in_=xg[:].rearrange("p g n j -> p (g n j)"),
            )

        def logits():
            out = psum("l", [P, 4, E], F32, "pz")
            for t in range(4):
                for k in range(8):
                    nc.tensor.matmul(
                        out[:, t, :],
                        lhsT=xg[:, k // 4, P * t : P * t + P, k % 4],
                        rhs=gt[:, k // 4, k % 4, :],
                        start=(k == 0),
                        stop=(k == 7),
                    )

        def c_columns():
            out = psum("c", [P, 4, P], BF16, "pz")
            for t in range(4):
                nc.tensor.transpose(out[:, t, :], crow[:, t : R : 4], identb[:])
            nc.vector.tensor_copy(out=cf[:].rearrange("p e t -> p t e"), in_=out[:, :, 0:E])

        def softmax(step):
            if step == "sa":
                nc.vector.reduce_max(out=mx[:], in_=bank["l"][:], axis=AX.X)
            elif step == "sb0":
                nc.vector.tensor_tensor(
                    out=dl[:], in0=bank["l"][:], in1=mx[:].unsqueeze(2).to_broadcast([P, 4, E]), op=ALU.subtract
                )
            elif step == "sb":
                nc.scalar.activation(out=ex[:], in_=dl[:], func=ACT.Exp)
            elif step == "sc0":
                nc.vector.reduce_sum(out=sm[:], in_=ex[:], axis=AX.X)
            elif step == "sc1":
                nc.vector.reciprocal(out=rc[:], in_=sm[:])
            else:
                nc.vector.tensor_tensor(out=gg[:], in0=ex[:], in1=rc[:].unsqueeze(2).to_broadcast([P, 4, E]), op=ALU.mult)

        def mm1(e, t):
            out = psum(("p", e, t), [P, N], F32, "pa")
            for g in range(2):
                s = slice(R * g + P * t, R * g + P * t + P)
                nc.tensor.matmul_mx(
                    out=out[:],
                    lhsT=codes["v", e][:, s].bitcast(FP8X4),
                    lhsT_scale=scales["v", e][:, s],
                    rhs=xc[:, g, :].bitcast(FP8X4),
                    rhs_scale=xs[:, g, :],
                    start=(g == 0),
                    stop=(g == 1),
                )

        def tanh(e, t):
            out = tile_of(pt, e, [P, 4, N], F32, "pt", PB)
            nc.scalar.activation(out=out[:, t, :], in_=bank["p", e, t][:], func=ACT.Tanh)

        def cm_s(e, t):
            out = tile_of(qt, e, [P, 4, N], BF16, "qt", 2)
            nc.scalar.activation(out=out[:, t, :], in_=pt[e][:, t, :], func=ACT.Copy, scale=cf[:, e, t : t + 1])

        def prod(e):
            out = tile_of(qb, e, [P, N * 4], BF16, "qb", 2)
            if e in SCM:
                nc.vector.tensor_copy(
                    out=out[:].rearrange("p (c i t) -> p c t i", i=4, t=4), in_=qt[e][:].rearrange("p t (c i) -> p c t i", i=4)
                )
            else:
                nc.vector.tensor_tensor(
                    out=out[:].rearrange("p (c i t) -> p c t i", i=2, t=4),
                    in0=pt[e][:].rearrange("p t (c i) -> p c t i", i=2),
                    in1=cf[:, e, :].unsqueeze(1).unsqueeze(3).to_broadcast([P, 256, 4, 2]),
                    op=ALU.mult,
                )

        def q_q(e):
            quantize(("q", e), N, qb[e][:], 4)

        def mm2(e, t, h):
            out = psum(("z", e, t, h), [P, 512], F32, "pz")
            rows = slice(P * t, P * t + P)
            cols = slice(512 * h, 512 * h + 512)
            nc.tensor.matmul_mx(
                out=out[:],
                lhsT=codes["q", e][:, rows].bitcast(FP8X4),
                lhsT_scale=scales["q", e][:, rows],
                rhs=codes["u", e][:, cols].bitcast(FP8X4),
                rhs_scale=scales["u", e][:, cols],
                start=True,
                stop=True,
            )

        def before(e, t, h):
            s = slice(512 * h, 512 * h + 512)
            return bb[:, s] if e == 0 else acc[:, t, s]

        def mix(e, t, h):
            nc.vector.scalar_tensor_tensor(
                out=acc[:, t, 512 * h : 512 * h + 512],
                in0=bank["z", e, t, h][:],
                scalar=gg[:, t, e : e + 1],
                in1=before(e, t, h),
                op0=ALU.mult,
                op1=ALU.add,
            )

        def scale_z(e, t, h):
            out = tile_of(zg, (e, t, h), [P, 512], F32, "zg", 3)
            nc.scalar.activation(out=out[:], in_=bank["z", e, t, h][:], func=ACT.Copy, scale=gg[:, t, e : e + 1])

        def add_z(e, t, h):
            nc.gpsimd.tensor_tensor(out=acc[:, t, 512 * h : 512 * h + 512], in0=zg[e, t, h][:], in1=before(e, t, h), op=ALU.add)

        def fin(t, h, eng=nc.vector):
            s = slice(512 * h, 512 * h + 512)
            eng.tensor_tensor(out=acc[:, t, s], in0=acc[:, t, s], in1=x0t[:, t, s], op=ALU.mult)
            nc.sync.dma_start(out=out_0[P * t : P * t + P, s], in_=acc[:, t, s])

        def cast_y(t, h):
            s = slice(512 * h, 512 * h + 512)
            nc.scalar.copy(out=tile_of(yb, t, [P, D], BF16, "yb", 4)[:, s], in_=acc[:, t, s])

        def tr_y(t):
            out = psum(("y", t), [P, 4, P], F32, "pa")
            words = yb[t][:].bitcast(F32)
            for g in range(2):
                for w in range(2):
                    nc.tensor.transpose(out[:, 2 * g + w, :], words[:, 256 * g + w : 256 * g + 256 : 2], ident[:])

        def cp_y(t, eng):
            out = tile_of(yg, t, [P, 2, P, 4], BF16, "yg", 2)
            copy_on(eng, out[:].bitcast(F32), bank["y", t][:].rearrange("p (g w) r -> p g r w", g=2))

        def q_y(t):
            s = slice(P * t, P * t + P)
            for g in range(2):
                nc.vector.quantize_mx(
                    out=yc[:, g, s].bitcast(FP8X4),
                    scales=ys[:, g, s],
                    in_=yg[t][:, g, :, :].rearrange("p n j -> p (n j)"),
                )
            nc.sync.dma_start(
                out=out_1.bitcast(I32)[:, :, s, :].rearrange("g p m o -> p g (m o)"), in_=yc[:, :, s].bitcast(I32)
            )

        def store_scales():
            for q in range(4):
                queue = (nc.sync, nc.scalar)[q % 2]
                queue.dma_start(
                    out=out_2.bitcast(I32)[:, 4 * q : 4 * q + 4, :].rearrange("g q m -> q g m"),
                    in_=ys[32 * q : 32 * q + 4, :, :].bitcast(I32),
                )

        nc.vector.memset(warm[:], 0.0)
        nc.vector.memset(crow[:], 0.0)
        nc.scalar.activation(out=warm[:, 1:2], in_=warm[:, 0:1], func=ACT.Exp)
        make_identity(nc, ident[:])
        nc.gpsimd.tensor_copy(out=identb[:], in_=ident[:])
        nc.scalar.dma_start(out=crow[0:E, :], in_=c)
        load_x(0)
        load_x(1)
        load_v(0, 0)
        load_x(2)
        load_x(3)
        load_v(0, 1)
        nc.sync.dma_start(out=gt[:].rearrange("p g t e -> p g (t e)"), in_=gate.rearrange("(g p t) e -> p g (t e)", g=2, t=4))
        load_v(1, 0)
        load_u(0)
        load_u(1)
        load_v(2, 0)
        load_u(2)
        load_v(3, 0)
        nc.sync.dma_start(out=bb[:], in_=b.partition_broadcast(P))
        load_u(3)
        tr_x(0)
        il_v(0, 0, "V")
        cp_x(0, "S")
        tr_x(1)
        cp_x(1, "S")
        tr_x(2)
        cp_x(2, "S")
        il_v(0, 1, "V")
        tr_x(3)
        x0t = keep([P, 4, D], BF16, "rows")
        nc.sync.dma_start(out=x0t[:], in_=x0.rearrange("(s p) d -> p s d", p=P))
        cp_x(3, "S")
        q_x()
        c_columns()
        logits()
        q_w("v", 0)
        il_v(1, 1, "S")
        il_u(0, 1, "S")
        il_v(1, 0, "V")
        il_u(0, 0, "V")
        mm1(0, 1)
        q_w("v", 1)
        softmax("sa")
        tanh(0, 1)
        mm1(0, 3)
        tanh(0, 3)
        mm1(0, 2)
        il_u(1, 1, "V")
        tanh(0, 2)
        mm1(0, 0)
        tanh(0, 0)
        mm1(1, 3)
        tanh(1, 3)
        cm_s(1, 3)
        q_w("u", 0)
        softmax("sb0")
        softmax("sb")
        mm1(1, 1)
        tanh(1, 1)
        mm1(1, 2)
        tanh(1, 2)
        cm_s(1, 1)
        pe_il("v", 2, 1, 1)
        pe_il("v", 2, 1, 0)
        pe_cp("v", 2, 1, 1)
        prod(0)
        il_v(2, 0, "V")
        softmax("sc0")
        q_q(0)
        mm2(0, 0, 0)
        pe_cp("v", 2, 1, 0)
        pe_il("v", 3, 0, 0)
        softmax("sc1")
        il_u(1, 0, "S")
        il_v(3, 1, "V")
        mm1(1, 0)
        cm_s(1, 2)
        q_w("v", 2)
        softmax("sc")
        q_w("u", 1)
        pe_il("v", 3, 0, 1)
        mm2(0, 1, 0)
        pe_cp("v", 3, 0, 0)
        mm2(0, 3, 0)
        mm2(0, 0, 1)
        mix(0, 0, 0)
        il_u(2, 0, "V")
        pe_cp("v", 3, 0, 1)
        tanh(1, 0)
        cm_s(1, 0)
        prod(1)
        mix(0, 1, 0)
        mm2(0, 1, 1)
        mm1(2, 2)
        tanh(2, 2)
        pe_il("u", 2, 1, 1)
        pe_cp("u", 2, 1, 1)
        mm1(2, 1)
        tanh(2, 1)
        cm_s(2, 1)
        q_q(1)
        mm1(2, 3)
        tanh(2, 3)
        cm_s(2, 3)
        cm_s(2, 2)
        q_w("v", 3)
        mm2(0, 2, 1)
        mix(0, 3, 0)
        pe_il("u", 2, 1, 0)
        pe_cp("u", 2, 1, 0)
        mm1(2, 0)
        mm2(1, 0, 1)
        mm1(3, 2)
        tanh(3, 2)
        mix(0, 1, 1)
        mix(0, 0, 1)
        mm1(3, 1)
        mix(0, 2, 1)
        mix(1, 0, 1)
        il_u(3, 0, "S")
        mm1(3, 0)
        q_w("u", 2)
        mm2(1, 1, 0)
        tanh(2, 0)
        mm2(1, 3, 0)
        mix(1, 3, 0)
        mm2(0, 3, 1)
        mix(1, 1, 0)
        mm2(1, 1, 1)
        mix(1, 1, 1)
        mm2(0, 2, 0)
        cm_s(2, 0)
        mm2(1, 3, 1)
        tanh(3, 0)
        cm_s(3, 0)
        mix(0, 3, 1)
        pe_il("u", 3, 1, 0)
        prod(2)
        mix(1, 3, 1)
        mm1(3, 3)
        tanh(3, 3)
        pe_cp("u", 3, 1, 0)
        tanh(3, 1)
        q_q(2)
        mm2(2, 3, 1)
        cm_s(3, 3)
        mix(0, 2, 0)
        mix(2, 3, 1)
        mm2(2, 0, 1)
        cm_s(3, 2)
        mm2(2, 3, 0)
        mix(2, 0, 1)
        mm2(1, 2, 0)
        mm2(2, 1, 0)
        mm2(2, 1, 1)
        mix(2, 3, 0)
        pe_il("u", 3, 1, 1)
        cm_s(3, 1)
        mix(2, 1, 0)
        mix(1, 2, 0)
        prod(3)
        pe_cp("u", 3, 1, 1)
        q_w("u", 3)
        q_q(3)
        mm2(1, 0, 0)
        mix(1, 0, 0)
        mm2(3, 1, 0)
        mm2(3, 0, 1)
        mix(2, 1, 1)
        mm2(3, 3, 0)
        mix(3, 1, 0)
        mix(3, 0, 1)
        mix(3, 3, 0)
        fin(1, 0)
        mm2(3, 3, 1)
        mix(3, 3, 1)
        mm2(2, 0, 0)
        cast_y(1, 0)
        mm2(3, 1, 1)
        mix(3, 1, 1)
        fin(0, 1)
        mm2(1, 2, 1)
        mix(1, 2, 1)
        fin(3, 0)
        mm2(2, 2, 1)
        cast_y(0, 1)
        fin(1, 1)
        cast_y(1, 1)
        mix(2, 0, 0)
        fin(3, 1)
        cast_y(3, 1)
        cast_y(3, 0)
        mix(2, 2, 1)
        mm2(3, 0, 0)
        mix(3, 0, 0)
        mm2(2, 2, 0)
        mix(2, 2, 0)
        tr_y(1)
        fin(0, 0)
        mm2(3, 2, 0)
        cp_y(1, "S")
        cast_y(0, 0)
        mm2(3, 2, 1)
        tr_y(3)
        mix(3, 2, 0)
        tr_y(0)
        cp_y(3, "S")
        mix(3, 2, 1)
        fin(2, 0)
        fin(2, 1)
        q_y(1)
        cp_y(0, "V")
        cast_y(2, 0)
        q_y(3)
        q_y(0)
        cast_y(2, 1)
        tr_y(2)
        cp_y(2, "S")
        q_y(2)
        store_scales()
